import numpy as np, ml_dtypes
CORES = [113,118,241,246]
N = 4
BF = ml_dtypes.bfloat16
def gentries(a):
    return np.ascontiguousarray(a.reshape(8, 16, -1).transpose(0, 2, 1)).reshape(8, -1)
def gtable(e):
    e = np.asarray(e); return np.ascontiguousarray(e.reshape(8, -1, 16).transpose(0, 2, 1)).reshape(128, -1).astype(np.int32)
M, Q, V, TOP = 2048, 256, 4, 15
WT = 15
def far_maps(rng):
    p = np.argsort(rng.random((N, 8, M)), axis=-1)
    return np.where(rng.random(p.shape) < 0.125, rng.integers(0, M, p.shape), p).astype(np.int32)
def lists(a):
    return np.stack([gtable(u) for u in a])
def setup_inputs(rng):
    return {"nx": far_maps(rng), "w": rng.integers(0, WT + 1, (N, 8, M)).astype(np.int32), "x": lists(rng.integers(0, M, (N, 8, Q))), "e": lists(rng.integers(0, TOP + 1, (N, 8, V * Q)))}
def setup_inputs_ends(rng):
    d = setup_inputs(rng); k = rng.choice(np.array([0, TOP]), (N, 8, V, Q))
    k[:, :, :, 0] = 0; k[:, :, :, 1] = TOP; k[:, :, :, Q - 1] = 0; k[:, :, V - 1, Q - 1] = TOP
    d["e"] = lists(k.reshape(N, 8, V * Q))
    w = np.where(rng.random((N, 8, M)) < 0.5, WT, 0); w[:, 0] = WT; d["w"] = w.astype(np.int32)
    return d
def setup_inputs_still(rng):
    d = setup_inputs(rng); a = np.array(d["nx"]); s = int(rng.integers(0, 4)); p = np.arange(M)
    for r in range(N):
        h = (r + s) % 4; c = rng.choice(np.arange(2, M - 1), 8, replace=False)
        if h == 0:
            a[r] = p
        elif h == 1:
            c[0] = 0; c[1] = M - 1; a[r] = rng.permutation(c)[:, None]
        elif h == 2:
            c[0] = 1; c[1] = M - 1; a[r] = (p + rng.permutation(c)[:, None]) % M
        else:
            c[0] = 1; c[1] = M - 1; a[r] = p ^ rng.permutation(c)[:, None]
    d["nx"] = a; return d
def setup_inputs_alike(rng):
    d = setup_inputs(rng); k = rng.integers(0, TOP + 1, (N, 8, V, Q // 2))
    z = np.where((np.arange(N)[:, None] + np.arange(8)) % 2 == 0, M - 1, 0)
    d["x"] = lists(np.repeat(z[:, :, None], Q, axis=2)); d["e"] = lists(np.concatenate([k, k], -1).reshape(N, 8, V * Q)); return d
def setup_inputs_spread(rng):
    d = setup_inputs(rng)
    d["nx"] = np.floor(M * rng.random((N, 8, M)) ** 3).astype(np.int32)
    d["w"] = np.floor((WT + 1) * rng.random((N, 8, M)) ** 4).astype(np.int32)
    d["x"] = lists(np.floor(M * rng.random((N, 8, Q)) ** 2)); d["e"] = lists(np.floor((TOP + 1) * rng.random((N, 8, V * Q)) ** 3)); return d
def check_inputs(d):
    bad = []
    for name, top in (("nx", M - 1), ("w", WT), ("x", M - 1), ("e", TOP)):
        if np.min(d[name]) < 0 or np.max(d[name]) > top: bad.append("range of " + name)
    return bad
def reference(nx, w, x, e):
    last = np.zeros((N, 128, Q // 16), np.int32); total = np.zeros((N, 128, Q // 16), np.int32); g = np.arange(8)[:, None]
    for r in range(N):
        p = gentries(x[r]).astype(np.int64); k = gentries(e[r]).reshape(8, V, Q); s = np.zeros((8, Q), np.int64)
        for t in range(V):
            q = (r + t) % N
            for i in range(TOP):
                go = i < k[:, t]
                s = s + np.where(go, w[q][g, p], 0)
                p = np.where(go, nx[q][g, p], p)
        last[r] = gtable(p); total[r] = gtable(s)
    return {"last": np.asarray(last, np.float32), "total": np.asarray(total, np.float32)}

@@ -1,0 +1,253 @@
+from concourse.mybir import AluOpType as A, ActivationFunctionType as AF
+
+CAP = [3, 4, 5, 5]
+NS = [5, 4, 3, 3]
+N0 = [0, 5, 9, 12, 15]
+NV = 4
+BIG = 8388608.0
+SELU = 1048576.0
+
+SCRATCH = {"ps%d" % b: ("psum", [128, 512], "float32") for b in range(8)}
+for _dt, _bufs in (
+        ("int32", "srci 512 pidx 8 p31 8 p15 8 lst 144 lb 144 ei 64 hi 192 ha 192 fi 16 fa 16 fb 16 t2 16 t3 16"),
+        ("float16", "s16 512 lr 512"),
+        ("uint16", "l0 128 off 240"),
+        ("float32", "ic 512 f31 8 f15 8 valc 8 row16 16 b16 16 sd 256 lt 144 lx 144 ls 144 xp 16 xq 16 ef 64 rr 304 ad 256"
+                    " lad1 64 lad2 48 lad3 48 ex 3840 sc 3840 gt 256 win 12288 wts 2048 land1 16 land2 16 land3 16 fin 48"
+                    " vp1 64 vp2 48 vp3 48 hp 192 h96 96 h48 48 h16 16 acc 16 t1 16 ol 16 ot 16")):
+    _w = _bufs.split()
+    for _i in range(0, len(_w), 2):
+        SCRATCH[_w[_i]] = ("sbuf", [128, int(_w[_i + 1])], _dt)
+SEMAPHORES = ["v", "s", "pe", "gi", "lda", "ldb", "lde", "outs", "loc",
+              "ad1", "ad2", "ad3", "hop1", "hop2", "hop3", "hop4", "bg1", "bg2"]
+
+
+def rank_program(g, core, T, topo):
+    rank = T.rank_of(core)
+    if rank is None:
+        return
+    V, S, PE, Y = g.vector, g.scalar, g.tensor, g.sync
+    sem = T.sem
+    peer = lambda d: T.cores[(rank + d) % NV]
+    cnt = {"v": 0, "s": 0, "pe": 0, "gi": 0, "loc": 0}
+
+    def done(name, ins):
+        ins.then_inc(sem[name], 1)
+        cnt[name] += 1
+        return cnt[name]
+
+    def v(ins):
+        return done("v", ins)
+
+    def s(ins):
+        return done("s", ins)
+
+    def vw(n):
+        V.wait_ge(sem.v, n)
+
+    def ts(out, in0, op, c, op1=None, c1=None):
+        if op1 is None:
+            return v(V.tensor_scalar(out=out, in0=in0, scalar1=c, scalar2=None, op0=op))
+        return v(V.tensor_scalar(out=out, in0=in0, scalar1=c, scalar2=c1, op0=op, op1=op1))
+
+    def tt(out, in0, in1, op=A.add):
+        return v(V.tensor_tensor(out=out, in0=in0, in1=in1, op=op))
+
+    Y.dma_start(out=T.srci[32:64, :], in_=T.nx[:]).then_inc(sem.lda, 16)
+    Y.dma_start(out=T.srci[0:32, :], in_=T.nx[:]).then_inc(sem.lda, 16)
+    Y.dma_start(out=T.srci[64:96, :], in_=T.w[:]).then_inc(sem.lda, 16)
+    S.dma_start(out=T.ei[:, :], in_=T.e[:]).then_inc(sem.lde, 16)
+    S.dma_start(out=T.lst[:, 0:128], in_=T.nx[:]).then_inc(sem.ldb, 16)
+    S.dma_start(out=T.lst[:, 128:144], in_=T.x[:]).then_inc(sem.ldb, 16)
+
+    g_p = done("gi", g.iota(T.pidx[:, 0:1], [[0, 1]], 0, 1))
+    done("gi", g.iota(T.row16[:, :], [[1, 16]], 0, 0, allow_small_or_imprecise_dtypes=True))
+    g_ic = done("gi", g.iota(T.ic[:, :], [[1, 4], [4, 8], [0, 16]], 0, 0, allow_small_or_imprecise_dtypes=True))
+    g_id = done("gi", g.iota(T.win[:, 0:2048], [[512, 2048]], 0, 0, allow_small_or_imprecise_dtypes=True))
+
+    v(V.memset(T.valc[0:32, 0:1], 16.0))
+    v(V.memset(T.valc[32:64, 0:1], -2047.0))
+    v(V.memset(T.valc[64:96, 0:1], 1.0 / 512))
+    v(V.memset(T.ad[:, 240:256], 0.0))
+    for t in range(NV):
+        c0 = 16 * (N0[t] + t + NS[t])
+        v(V.memset(T.rr[:, c0:c0 + 16], 0.0))
+    n = v(V.memset(T.sd[:, :], 0.0))
+    vw(n)
+    v(V.memset(T.sd[:, 0:256:16], -BIG))
+    V.wait_ge(sem.gi, g_p)
+    ts(T.p31[:, 0:1], T.pidx[:, 0:1], A.bitwise_and, 31)
+    vw(ts(T.p15[:, 0:1], T.pidx[:, 0:1], A.bitwise_and, 15))
+    v(V.tensor_copy(out=T.f31[:, 0:1], in_=T.p31[:, 0:1]))
+    vw(v(V.tensor_copy(out=T.f15[:, 0:1], in_=T.p15[:, 0:1])))
+    V.wait_ge(sem.gi, g_ic)
+    ts(T.b16[:, :], T.row16[:, :], A.not_equal, T.f15[:, 0:1], A.mult, -BIG)
+    ts(T.lr[0:96, :], T.ic[0:96, :], A.is_equal, T.f31[0:96, 0:1], A.mult, T.valc[0:96, 0:1])
+
+    V.wait_ge(sem.lde, 16)
+    v_ef = v(V.tensor_copy(out=T.ef[:, :], in_=T.ei[:, :]))
+    V.wait_ge(sem.lda, 48)
+    v_half = []
+    for c0 in (0, 256):
+        half = T.srci[32:64, c0:c0 + 256]
+        vw(ts(half, half, A.arith_shift_right, 7))
+        v_half.append(v(V.tensor_copy(out=T.s16[0:96, c0:c0 + 256], in_=T.srci[0:96, c0:c0 + 256])))
+
+    for bank in range(8):
+        i2 = bank % 4
+        k0 = 0 if bank < 4 else 64
+        if bank in (0, 2):
+            PE.wait_ge(sem.v, v_half[bank // 2])
+        for h in range(4):
+            ins = PE.matmul(out=T["ps%d" % bank][:, 128 * h:128 * h + 128], lhsT=T.lr[k0:96, 128 * h:128 * h + 128],
+                            rhs=T.s16[k0:96, 128 * i2:128 * i2 + 128], start=True, stop=True)
+        done("pe", ins)
+
+    def evac(bank, on_vector):
+        (V if on_vector else S).wait_ge(sem.pe, bank + 1)
+        last = 0
+        for h in range(4):
+            i = 4 * h + bank % 4
+            out = T.win[:, 2048 + i:4096:16] if bank < 4 else T.wts[:, i:2048:16]
+            src = T["ps%d" % bank][:, 128 * h:128 * h + 128]
+            last = ts(out, src, A.mult, 512.0) if on_vector else s(S.activation(out=out, in_=src, func=AF.Copy, scale=512.0))
+        return last
+
+    S.wait_ge(sem.v, v_ef)
+    s_rr = 0
+    for t in range(NV):
+        for k in range(NS[t]):
+            c0 = 16 * (N0[t] + t + k)
+            s_rr = s(S.activation(out=T.rr[:, c0:c0 + 16], in_=T.ef[:, 16 * t:16 * t + 16], func=AF.Relu,
+                                  bias=-CAP[t] * k * SELU, scale=SELU))
+    s_ev = 0
+    for bank in (1, 3, 5, 7):
+        s_ev = evac(bank, False)
+
+    V.wait_ge(sem.ldb, 32)
+    n1 = ts(T.lb[:, :], T.lst[:, :], A.arith_shift_right, 7)
+    ts(T.lx[:, :], T.lst[:, :], A.mult, 16)
+    vw(n1)
+    vw(ts(T.lt[:, :], T.lb[:, :], A.mult, -2047))
+    vw(tt(T.ls[:, :], T.lt[:, :], T.lx[:, :]))
+    v(V.tensor_copy(out=T.l0[:, :], in_=T.ls[:, 0:128]))
+    ts(T.xp[:, :], T.ls[:, 128:144], A.mult, 512.0)
+    evac(0, True)
+    evac(2, True)
+    V.wait_ge(sem.s, s_rr)
+    v_ad = 0
+    for t in range(NV):
+        r0, w0 = 16 * (N0[t] + t), 16 * NS[t]
+        v_ad = tt(T.ad[:, 16 * N0[t]:16 * N0[t] + w0], T.rr[:, r0:r0 + w0], T.rr[:, r0 + 16:r0 + 16 + w0], A.subtract)
+    evac(4, True)
+    vw(v_ad)
+    tt(T.xq[:, :], T.xp[:, :], T.ad[:, 0:16])
+    v_b6 = evac(6, True)
+
+    def send(out, src, d, name):
+        dst = peer(d)
+        rid, pid = topo.addr(dst, core)
+        g.remote_dma(out, src, sem[name], sem.loc, pid, rid, topo.mask(core, dst))
+        cnt["loc"] += len(topo.engines(core, dst))
+
+    def landed(d):
+        return len(topo.engines(peer(-d), core))
+
+    g.wait_ge(sem.v, v_ad)
+    for t in (1, 2, 3):
+        send(T["lad%d" % t][:, :], T.ad[:, 16 * (N0[t] + 1):16 * (N0[t + 1] + 1)], t, "ad%d" % t)
+
+    s_ex = []
+    S.wait_ge(sem.v, v_ad)
+    for t in range(NV):
+        if t:
+            S.wait_ge(sem["ad%d" % t], landed(t))
+        src = T["lad%d" % t][:, :] if t else T.ad[:, 16:16 * (NS[0] + 1)]
+        last = 0
+        for i in range(16):
+            last = s(S.activation(out=T.ex[:, 256 * N0[t] + i:256 * N0[t + 1]:16], in_=src, func=AF.Identity,
+                                  bias=T.b16[:, i:i + 1]))
+        s_ex.append(last)
+
+    def power(k):
+        return tt(T.win[:, 2048 * k:2048 * (k + 1)], T.win[:, 2048 * (k - 1):2048 * k].indirect(T.l0[:, 0:128]), T.wts[:, :])
+
+    vw(v_b6)
+    V.wait_ge(sem.s, s_ev)
+    n = power(2)
+    ts(T.off[:, 0:16], T.xq[:, :], A.mult, 1.0 / 512)
+    vw(n)
+    vw(power(3))
+    V.wait_ge(sem.gi, g_id)
+
+    for t in range(NV):
+        if t:
+            V.wait_ge(sem["hop%d" % t], landed(1))
+            vw(ts(T.off[:, 16 * N0[t]:16 * N0[t] + 16], T["land%d" % t][:, :], A.mult, 1.0 / 512))
+        V.wait_ge(sem.s, s_ex[t])
+        H = T.hp if t == 0 else T["vp%d" % t]
+        n = 0
+        s_cp = 0
+        for k in range(NS[t]):
+            j = N0[t] + k
+            if k:
+                vw(ts(T.off[:, 16 * j:16 * j + 16], T.sc[:, 256 * j - 241:256 * j:16], A.mult, 1.0 / 512))
+            vw(tt(T.gt[:, :], T.win[:, 0:2048 * (CAP[t] + 1)].indirect(T.off[:, 16 * j:16 * j + 16]),
+                  T.ex[:, 256 * j:256 * j + 256]))
+            n = v(V.tensor_tensor_scan(out=T.sc[:, 256 * j:256 * j + 256], data0=T.sd[:, :], data1=T.gt[:, :],
+                                       initial=0.0, op0=A.add, op1=A.max))
+            vw(n)
+            res = T.sc[:, 256 * j + 15:256 * j + 256:16]
+            if k < NS[t] - 1:
+                S.wait_ge(sem.v, n)
+                s_cp = s(S.activation(out=H[:, 16 * k:16 * k + 16], in_=res, func=AF.Copy))
+            else:
+                n = v(V.tensor_copy(out=H[:, 16 * k:16 * k + 16], in_=res))
+        g.wait_ge(sem.v, n)
+        if t < 3:
+            e0 = 16 * (NS[t] - 1)
+            send(T["land%d" % (t + 1)][:, :], H[:, e0:e0 + 16], 1, "hop%d" % (t + 1))
+            if t:
+                g.wait_ge(sem.s, s_cp)
+                send(T.hp[:, 16 * N0[t]:16 * N0[t + 1]], H[:, :], -t, "bg%d" % t)
+            else:
+                s_cp0, v_cp0 = s_cp, n
+        else:
+            g.wait_ge(sem.s, s_cp)
+            send(T.fin[:, :], H[:, :], 1, "hop4")
+        if t < 2:
+            vw(power(t + 4))
+
+    V.wait_ge(sem.s, s_cp0)
+    vw(v_cp0)
+    V.wait_ge(sem.bg1, landed(-1))
+    V.wait_ge(sem.bg2, landed(-2))
+    vw(v(V.tensor_copy(out=T.hi[:, :], in_=T.hp[:, :])))
+    vw(ts(T.ha[:, :], T.hi[:, :], A.bitwise_and, 511))
+    vw(tt(T.h96[:, :], T.ha[:, 0:96], T.ha[:, 96:192]))
+    vw(tt(T.h48[:, :], T.h96[:, 0:48], T.h96[:, 48:96]))
+    vw(tt(T.h16[:, :], T.h48[:, 0:16], T.h48[:, 16:32]))
+    vw(tt(T.acc[:, :], T.h16[:, :], T.h48[:, 32:48]))
+
+    V.wait_ge(sem.hop4, landed(1))
+    n1 = tt(T.t1[:, :], T.fin[:, 0:16], T.fin[:, 16:32])
+    n2 = v(V.tensor_copy(out=T.fi[:, :], in_=T.fin[:, 32:48]))
+    vw(n1)
+    n3 = tt(T.t2[:, :], T.t1[:, :], T.fin[:, 32:48])
+    vw(n2)
+    ts(T.fb[:, :], T.fi[:, :], A.bitwise_and, 7680, A.arith_shift_right, 2)
+    vw(n3)
+    n5 = ts(T.t3[:, :], T.t2[:, :], A.bitwise_and, 511)
+    n6 = ts(T.fa[:, :], T.fi[:, :], A.arith_shift_right, 13)
+    vw(n5)
+    v_t = tt(T.ot[:, :], T.t3[:, :], T.acc[:, :])
+    vw(n6)
+    v_l = tt(T.ol[:, :], T.fa[:, :], T.fb[:, :])
+    S.wait_ge(sem.v, v_t)
+    S.dma_start(out=T.total[:], in_=T.ot[:, :]).then_inc(sem.outs, 16)
+    Y.wait_ge(sem.v, v_l)
+    Y.dma_start(out=T.last[:], in_=T.ol[:, :]).then_inc(sem.outs, 16)
+
+    for name in ("loc", "v", "s", "pe", "gi"):
+        g.wait_ge(sem[name], cnt[name])
+    g.wait_ge(sem.outs, 32)

@@ -7,14 +7,16 @@ NV = 4
 BIG = 8388608.0
 SELU = 1048576.0
 
-SCRATCH = {"ps%d" % b: ("psum", [128, 512], "float32") for b in range(8)}
+SCRATCH = {"ps%d" % b: ("psum", [128, 32, 16], "float32") for b in range(8)}
+SCRATCH["srci"] = ("sbuf", [128, 4, 128], "int32")
+SCRATCH["s16"] = ("sbuf", [128, 128, 4], "float16")
 for _dt, _bufs in (
-        ("int32", "srci 512 pidx 8 p31 8 p15 8 lst 144 lb 144 ei 64 hi 192 ha 192 fi 16 fa 16 fb 16 t2 16 t3 16"),
-        ("float16", "s16 512 lr 512"),
-        ("uint16", "l0 128 off 240"),
-        ("float32", "ic 512 f31 8 f15 8 valc 8 row16 16 b16 16 sd 256 lt 144 lx 144 ls 144 xp 16 xq 16 ef 64 rr 304 ad 256"
-                    " lad1 64 lad2 48 lad3 48 ex 3840 sc 3840 gt 256 win 12288 wts 2048 land1 16 land2 16 land3 16 fin 48"
-                    " vp1 64 vp2 48 vp3 48 hp 192 h96 96 h48 48 h16 16 acc 16 t1 16 ol 16 ot 16")):
+        ("int32", "pidx 8 p31 8 p15 8 lst 144 lb 144 ei 64 hi 192 ha 192 fo 32 fin 32 fa 16 fb 16 t2 16 t3 16"),
+        ("float16", "lr 512"),
+        ("uint16", "l0 128 off 240 ho0 16 ho1 16 ho2 16 land1 16 land2 16 land3 16"),
+        ("float32", "ic 512 f31 8 f15 8 valc 8 row16 16 b16 16 sd 256 lt 144 lx 144 ls 144 xp 16 xq 16 ef 64"
+                    " le1 32 le2 32 le3 16 rr 240 uu 256 ad 256 ex 3840 sc 3840 gt 256 win 12288 wts 1024 tmp 2048"
+                    " vp1 64 vp2 48 hp 192 h96 96 h48 48 h16 16 acc 16 ol 16 ot 16")):
     _w = _bufs.split()
     for _i in range(0, len(_w), 2):
         SCRATCH[_w[_i]] = ("sbuf", [128, int(_w[_i + 1])], _dt)
@@ -39,9 +41,6 @@ def rank_program(g, core, T, topo):
     def v(ins):
         return done("v", ins)
 
-    def s(ins):
-        return done("s", ins)
-
     def vw(n):
         V.wait_ge(sem.v, n)
 
@@ -53,9 +52,15 @@ def rank_program(g, core, T, topo):
     def tt(out, in0, in1, op=A.add):
         return v(V.tensor_tensor(out=out, in0=in0, in1=in1, op=op))
 
-    Y.dma_start(out=T.srci[32:64, :], in_=T.nx[:]).then_inc(sem.lda, 16)
-    Y.dma_start(out=T.srci[0:32, :], in_=T.nx[:]).then_inc(sem.lda, 16)
-    Y.dma_start(out=T.srci[64:96, :], in_=T.w[:]).then_inc(sem.lda, 16)
+    def vcopy(out, in_):
+        return v(V.tensor_copy(out=out, in_=in_))
+
+    def act(out, in_, func=AF.Copy, bias=0.0, scale=1.0):
+        return done("s", S.activation(out=out, in_=in_, func=func, bias=bias, scale=scale))
+
+    Y.dma_start(out=T.srci[32:64, :, :], in_=T.nx[:]).then_inc(sem.lda, 16)
+    Y.dma_start(out=T.srci[0:32, :, :], in_=T.nx[:]).then_inc(sem.lda, 16)
+    Y.dma_start(out=T.srci[64:96, :, :], in_=T.w[:]).then_inc(sem.lda, 16)
     S.dma_start(out=T.ei[:, :], in_=T.e[:]).then_inc(sem.lde, 16)
     S.dma_start(out=T.lst[:, 0:128], in_=T.nx[:]).then_inc(sem.ldb, 16)
     S.dma_start(out=T.lst[:, 128:144], in_=T.x[:]).then_inc(sem.ldb, 16)
@@ -65,84 +70,49 @@ def rank_program(g, core, T, topo):
     g_ic = done("gi", g.iota(T.ic[:, :], [[1, 4], [4, 8], [0, 16]], 0, 0, allow_small_or_imprecise_dtypes=True))
     g_id = done("gi", g.iota(T.win[:, 0:2048], [[512, 2048]], 0, 0, allow_small_or_imprecise_dtypes=True))
 
-    v(V.memset(T.valc[0:32, 0:1], 16.0))
-    v(V.memset(T.valc[32:64, 0:1], -2047.0))
-    v(V.memset(T.valc[64:96, 0:1], 1.0 / 512))
+    v(V.memset(T.valc[0:32, 0:1], 8192.0))
+    v(V.memset(T.valc[32:64, 0:1], -8188.0))
+    v(V.memset(T.valc[64:96, 0:1], 1.0))
     v(V.memset(T.ad[:, 240:256], 0.0))
-    for t in range(NV):
-        c0 = 16 * (N0[t] + t + NS[t])
-        v(V.memset(T.rr[:, c0:c0 + 16], 0.0))
     n = v(V.memset(T.sd[:, :], 0.0))
     vw(n)
     v(V.memset(T.sd[:, 0:256:16], -BIG))
     V.wait_ge(sem.gi, g_p)
     ts(T.p31[:, 0:1], T.pidx[:, 0:1], A.bitwise_and, 31)
     vw(ts(T.p15[:, 0:1], T.pidx[:, 0:1], A.bitwise_and, 15))
-    v(V.tensor_copy(out=T.f31[:, 0:1], in_=T.p31[:, 0:1]))
-    vw(v(V.tensor_copy(out=T.f15[:, 0:1], in_=T.p15[:, 0:1])))
+    vcopy(T.f31[:, 0:1], T.p31[:, 0:1])
+    vw(vcopy(T.f15[:, 0:1], T.p15[:, 0:1]))
     V.wait_ge(sem.gi, g_ic)
     ts(T.b16[:, :], T.row16[:, :], A.not_equal, T.f15[:, 0:1], A.mult, -BIG)
     ts(T.lr[0:96, :], T.ic[0:96, :], A.is_equal, T.f31[0:96, 0:1], A.mult, T.valc[0:96, 0:1])
 
     V.wait_ge(sem.lde, 16)
-    v_ef = v(V.tensor_copy(out=T.ef[:, :], in_=T.ei[:, :]))
+    v_ef = vcopy(T.ef[:, :], T.ei[:, :])
     V.wait_ge(sem.lda, 48)
     v_half = []
-    for c0 in (0, 256):
-        half = T.srci[32:64, c0:c0 + 256]
-        vw(ts(half, half, A.arith_shift_right, 7))
-        v_half.append(v(V.tensor_copy(out=T.s16[0:96, c0:c0 + 256], in_=T.srci[0:96, c0:c0 + 256])))
+    for c0 in (0, 64):
+        half = T.srci[32:64, :, c0:c0 + 64]
+        vw(ts(half, half, A.bitwise_and, 1920))
+        n = 0
+        for i2 in range(4):
+            n = vcopy(T.s16[0:96, c0:c0 + 64, i2], T.srci[0:96, i2, c0:c0 + 64])
+        v_half.append(n)
 
     for bank in range(8):
-        i2 = bank % 4
+        c0 = 32 * (bank % 4)
         k0 = 0 if bank < 4 else 64
         if bank in (0, 2):
             PE.wait_ge(sem.v, v_half[bank // 2])
         for h in range(4):
-            ins = PE.matmul(out=T["ps%d" % bank][:, 128 * h:128 * h + 128], lhsT=T.lr[k0:96, 128 * h:128 * h + 128],
-                            rhs=T.s16[k0:96, 128 * i2:128 * i2 + 128], start=True, stop=True)
+            ins = PE.matmul(out=T["ps%d" % bank][:, :, 4 * h:4 * h + 4], lhsT=T.lr[k0:96, 128 * h:128 * h + 128],
+                            rhs=T.s16[k0:96, c0:c0 + 32, :], start=True, stop=True)
         done("pe", ins)
 
     def evac(bank, on_vector):
         (V if on_vector else S).wait_ge(sem.pe, bank + 1)
-        last = 0
-        for h in range(4):
-            i = 4 * h + bank % 4
-            out = T.win[:, 2048 + i:4096:16] if bank < 4 else T.wts[:, i:2048:16]
-            src = T["ps%d" % bank][:, 128 * h:128 * h + 128]
-            last = ts(out, src, A.mult, 512.0) if on_vector else s(S.activation(out=out, in_=src, func=AF.Copy, scale=512.0))
-        return last
-
-    S.wait_ge(sem.v, v_ef)
-    s_rr = 0
-    for t in range(NV):
-        for k in range(NS[t]):
-            c0 = 16 * (N0[t] + t + k)
-            s_rr = s(S.activation(out=T.rr[:, c0:c0 + 16], in_=T.ef[:, 16 * t:16 * t + 16], func=AF.Relu,
-                                  bias=-CAP[t] * k * SELU, scale=SELU))
-    s_ev = 0
-    for bank in (1, 3, 5, 7):
-        s_ev = evac(bank, False)
-
-    V.wait_ge(sem.ldb, 32)
-    n1 = ts(T.lb[:, :], T.lst[:, :], A.arith_shift_right, 7)
-    ts(T.lx[:, :], T.lst[:, :], A.mult, 16)
-    vw(n1)
-    vw(ts(T.lt[:, :], T.lb[:, :], A.mult, -2047))
-    vw(tt(T.ls[:, :], T.lt[:, :], T.lx[:, :]))
-    v(V.tensor_copy(out=T.l0[:, :], in_=T.ls[:, 0:128]))
-    ts(T.xp[:, :], T.ls[:, 128:144], A.mult, 512.0)
-    evac(0, True)
-    evac(2, True)
-    V.wait_ge(sem.s, s_rr)
-    v_ad = 0
-    for t in range(NV):
-        r0, w0 = 16 * (N0[t] + t), 16 * NS[t]
-        v_ad = tt(T.ad[:, 16 * N0[t]:16 * N0[t] + w0], T.rr[:, r0:r0 + w0], T.rr[:, r0 + 16:r0 + 16 + w0], A.subtract)
-    evac(4, True)
-    vw(v_ad)
-    tt(T.xq[:, :], T.xp[:, :], T.ad[:, 0:16])
-    v_b6 = evac(6, True)
+        q0 = 512 * (bank % 4)
+        out = T.win[:, 2048 + q0:2560 + q0] if bank < 4 else T.wts[:, q0:q0 + 512]
+        return (vcopy if on_vector else act)(out, T["ps%d" % bank][:, :, :])
 
     def send(out, src, d, name):
         dst = peer(d)
@@ -153,76 +123,175 @@ def rank_program(g, core, T, topo):
     def landed(d):
         return len(topo.engines(peer(-d), core))
 
-    g.wait_ge(sem.v, v_ad)
+    g.wait_ge(sem.v, v_ef)
     for t in (1, 2, 3):
-        send(T["lad%d" % t][:, :], T.ad[:, 16 * (N0[t] + 1):16 * (N0[t + 1] + 1)], t, "ad%d" % t)
+        send(T["le%d" % t][:, :], T.ef[:, 16 * t:min(16 * t + 32, 64)], t, "ad%d" % t)
 
-    s_ex = []
-    S.wait_ge(sem.v, v_ad)
-    for t in range(NV):
-        if t:
-            S.wait_ge(sem["ad%d" % t], landed(t))
-        src = T["lad%d" % t][:, :] if t else T.ad[:, 16:16 * (NS[0] + 1)]
-        last = 0
-        for i in range(16):
-            last = s(S.activation(out=T.ex[:, 256 * N0[t] + i:256 * N0[t + 1]:16], in_=src, func=AF.Identity,
-                                  bias=T.b16[:, i:i + 1]))
-        s_ex.append(last)
+    def selectors(t, E):
+        m, k1 = CAP[t] * SELU, 1 if t else 0
+        a, b = 16 * (N0[t] + k1), 16 * N0[t + 1]
+        n = 0
+        for k in range(k1, NS[t]):
+            c = 16 * (N0[t] + k)
+            n = act(T.rr[:, c:c + 16], E[:, 0:16], AF.Relu, -m * k, SELU)
+        m2, n2 = 0, 0
+        if t < 3:
+            m2 = CAP[t + 1] * SELU
+            n2 = act(T.uu[:, b:b + 16], E[:, 16:32], AF.Relu, m2, -SELU)
+        S.wait_ge(sem.s, n)
+        n = act(T.uu[:, a:b], T.rr[:, a:b], AF.Relu, m, -1.0)
+        if t < 3:
+            S.wait_ge(sem.s, n2)
+            act(T.ad[:, b:b + 16], T.uu[:, b:b + 16], AF.Identity, m2, -1.0)
+        S.wait_ge(sem.s, n)
+        return act(T.ad[:, a:b], T.uu[:, a:b], AF.Identity, m, -1.0)
 
-    def power(k):
-        return tt(T.win[:, 2048 * k:2048 * (k + 1)], T.win[:, 2048 * (k - 1):2048 * k].indirect(T.l0[:, 0:128]), T.wts[:, :])
+    def expand(t, i0, i1):
+        n = 0
+        for i in range(i0, i1):
+            n = act(T.ex[:, 256 * N0[t] + i:256 * N0[t + 1]:16], T.ad[:, 16 * N0[t] + 16:16 * N0[t + 1] + 16], AF.Identity,
+                    T.b16[:, i:i + 1])
+        return n
 
-    vw(v_b6)
-    V.wait_ge(sem.s, s_ev)
-    n = power(2)
+    def raw(k, pieces):
+        out = {}
+        for q in pieces:
+            out[q] = act(T.tmp[:, 512 * q:512 * q + 512],
+                         T.win[:, 2048 * (k - 1):2048 * k].indirect(T.l0[:, 32 * q:32 * q + 32]))
+        return out
+
+    def add_w(k, pieces):
+        n = 0
+        for q in sorted(pieces):
+            V.wait_ge(sem.s, pieces[q])
+            c = 2048 * k + 512 * q
+            n = tt(T.win[:, c:c + 512], T.tmp[:, 512 * q:512 * q + 512], T["ps%d" % (4 + q)][:, :, :])
+        return n
+
+    def lower(k):
+        tt(T.win[:, 2048 * k:2048 * k + 1024], T.win[:, 2048 * (k - 1):2048 * k].indirect(T.l0[:, 0:64]), T.wts[:, :])
+
+    S.wait_ge(sem.v, v_ef)
+    s_ad = selectors(0, T.ef)
+    evac(1, False)
+    S.wait_ge(sem.s, s_ad)
+    expand(0, 0, 3)
+    s_r1 = evac(3, False)
+
+    V.wait_ge(sem.ldb, 32)
+    n1 = ts(T.lb[:, :], T.lst[:, :], A.arith_shift_right, 7)
+    ts(T.lx[:, :], T.lst[:, :], A.mult, 16)
+    vw(n1)
+    vw(ts(T.lt[:, :], T.lb[:, :], A.mult, -2047))
+    vw(tt(T.ls[:, :], T.lt[:, :], T.lx[:, :]))
+    vcopy(T.l0[:, :], T.ls[:, 0:128])
+    n1 = ts(T.xp[:, :], T.ls[:, 128:144], A.mult, 512.0)
+    evac(0, True)
+    v_r1 = evac(2, True)
+    vw(n1)
+    V.wait_ge(sem.s, s_ad)
+    n1 = tt(T.xq[:, :], T.xp[:, :], T.ad[:, 0:16])
+    evac(4, True)
+    vw(n1)
     ts(T.off[:, 0:16], T.xq[:, :], A.mult, 1.0 / 512)
+    v_w = evac(5, True)
+
+    S.wait_ge(sem.v, v_r1)
+    S.wait_ge(sem.s, s_r1)
+    part = raw(2, (2, 3))
+    expand(0, 3, 15)
+    vw(v_w)
+    V.wait_ge(sem.s, s_r1)
+    lower(2)
+    V.wait_ge(sem.pe, 8)
+    n = add_w(2, part)
+    S.wait_ge(sem.v, n)
+    part = raw(3, (2, 3))
+    s_ex0 = expand(0, 15, 16)
     vw(n)
-    vw(power(3))
+    lower(3)
+    n = add_w(3, part)
+    vw(n)
     V.wait_ge(sem.gi, g_id)
 
-    for t in range(NV):
+    def visitors(t):
+        S.wait_ge(sem["ad%d" % t], landed(t))
+        S.wait_ge(sem.s, selectors(t, T["le%d" % t]))
+        return expand(t, 0, 16)
+
+    S.wait_ge(sem.v, n)
+    part = raw(4, range(4))
+    s_ex1 = visitors(1)
+    s_ex2 = visitors(2)
+
+    def res(j):
+        return T.sc[:, 256 * j + 15:256 * j + 256:16]
+
+    def visit(t, s_ready):
+        V.wait_ge(sem.s, s_ready)
         if t:
             V.wait_ge(sem["hop%d" % t], landed(1))
-            vw(ts(T.off[:, 16 * N0[t]:16 * N0[t] + 16], T["land%d" % t][:, :], A.mult, 1.0 / 512))
-        V.wait_ge(sem.s, s_ex[t])
-        H = T.hp if t == 0 else T["vp%d" % t]
-        n = 0
-        s_cp = 0
+        marks = []
         for k in range(NS[t]):
             j = N0[t] + k
+            off = T["land%d" % t][:, 0:16] if t and k == 0 else T.off[:, 16 * j:16 * j + 16]
             if k:
-                vw(ts(T.off[:, 16 * j:16 * j + 16], T.sc[:, 256 * j - 241:256 * j:16], A.mult, 1.0 / 512))
-            vw(tt(T.gt[:, :], T.win[:, 0:2048 * (CAP[t] + 1)].indirect(T.off[:, 16 * j:16 * j + 16]),
-                  T.ex[:, 256 * j:256 * j + 256]))
+                n = ts(off, res(j - 1), A.mult, 1.0 / 512)
+                if j == 14:
+                    tt(T.fo[:, 16:32], res(12), res(13))
+                vw(n)
+            vw(tt(T.gt[:, :], T.win[:, 0:2048 * (CAP[t] + 1)].indirect(off), T.ex[:, 256 * j:256 * j + 256]))
             n = v(V.tensor_tensor_scan(out=T.sc[:, 256 * j:256 * j + 256], data0=T.sd[:, :], data1=T.gt[:, :],
                                        initial=0.0, op0=A.add, op1=A.max))
             vw(n)
-            res = T.sc[:, 256 * j + 15:256 * j + 256:16]
-            if k < NS[t] - 1:
-                S.wait_ge(sem.v, n)
-                s_cp = s(S.activation(out=H[:, 16 * k:16 * k + 16], in_=res, func=AF.Copy))
-            else:
-                n = v(V.tensor_copy(out=H[:, 16 * k:16 * k + 16], in_=res))
-        g.wait_ge(sem.v, n)
+            marks.append(n)
+        j = N0[t + 1] - 1
         if t < 3:
-            e0 = 16 * (NS[t] - 1)
-            send(T["land%d" % (t + 1)][:, :], H[:, e0:e0 + 16], 1, "hop%d" % (t + 1))
-            if t:
-                g.wait_ge(sem.s, s_cp)
-                send(T.hp[:, 16 * N0[t]:16 * N0[t + 1]], H[:, :], -t, "bg%d" % t)
-            else:
-                s_cp0, v_cp0 = s_cp, n
-        else:
-            g.wait_ge(sem.s, s_cp)
-            send(T.fin[:, :], H[:, :], 1, "hop4")
-        if t < 2:
-            vw(power(t + 4))
+            return marks, ts(T["ho%d" % t][:, :], res(j), A.mult, 1.0 / 512)
+        return marks, vcopy(T.fo[:, 0:16], res(j))
 
-    V.wait_ge(sem.s, s_cp0)
-    vw(v_cp0)
+    def hand_on(t, n):
+        g.wait_ge(sem.v, n)
+        send(T["land%d" % (t + 1)][:, :], T["ho%d" % t][:, :], 1, "hop%d" % (t + 1))
+
+    def keep(t, marks, H):
+        n = 0
+        for k, mark in enumerate(marks):
+            S.wait_ge(sem.v, mark)
+            n = act(H[:, 16 * k:16 * k + 16], res(N0[t] + k))
+        return n
+
+    def report(t, n):
+        g.wait_ge(sem.s, n)
+        send(T.hp[:, 16 * N0[t]:16 * N0[t + 1]], T["vp%d" % t][:, :], -t, "bg%d" % t)
+
+    marks, n = visit(0, s_ex0)
+    hand_on(0, n)
+    n = add_w(4, part)
+    vw(n)
+    S.wait_ge(sem.v, n)
+    part = raw(5, range(4))
+    s_own = keep(0, marks, T.hp)
+
+    marks, n = visit(1, s_ex1)
+    hand_on(1, n)
+    report(1, keep(1, marks, T.vp1))
+    n = add_w(5, part)
+    vw(n)
+    s_ex3 = visitors(3)
+
+    marks, n = visit(2, s_ex2)
+    hand_on(2, n)
+    report(2, keep(2, marks, T.vp2))
+
+    marks, n = visit(3, s_ex3)
+    g.wait_ge(sem.v, n)
+    send(T.fin[:, :], T.fo[:, :], 1, "hop4")
+
+    V.wait_ge(sem.s, s_own)
     V.wait_ge(sem.bg1, landed(-1))
     V.wait_ge(sem.bg2, landed(-2))
-    vw(v(V.tensor_copy(out=T.hi[:, :], in_=T.hp[:, :])))
+    vw(vcopy(T.hi[:, :], T.hp[:, :]))
     vw(ts(T.ha[:, :], T.hi[:, :], A.bitwise_and, 511))
     vw(tt(T.h96[:, :], T.ha[:, 0:96], T.ha[:, 96:192]))
     vw(tt(T.h48[:, :], T.h96[:, 0:48], T.h96[:, 48:96]))
@@ -230,23 +299,19 @@ def rank_program(g, core, T, topo):
     vw(tt(T.acc[:, :], T.h16[:, :], T.h48[:, 32:48]))
 
     V.wait_ge(sem.hop4, landed(1))
-    n1 = tt(T.t1[:, :], T.fin[:, 0:16], T.fin[:, 16:32])
-    n2 = v(V.tensor_copy(out=T.fi[:, :], in_=T.fin[:, 32:48]))
+    n1 = tt(T.t2[:, :], T.fin[:, 0:16], T.fin[:, 16:32])
+    ts(T.fb[:, :], T.fin[:, 0:16], A.bitwise_and, 7680, A.arith_shift_right, 2)
+    n2 = ts(T.fa[:, :], T.fin[:, 0:16], A.arith_shift_right, 13)
     vw(n1)
-    n3 = tt(T.t2[:, :], T.t1[:, :], T.fin[:, 32:48])
+    n1 = ts(T.t3[:, :], T.t2[:, :], A.bitwise_and, 511)
     vw(n2)
-    ts(T.fb[:, :], T.fi[:, :], A.bitwise_and, 7680, A.arith_shift_right, 2)
-    vw(n3)
-    n5 = ts(T.t3[:, :], T.t2[:, :], A.bitwise_and, 511)
-    n6 = ts(T.fa[:, :], T.fi[:, :], A.arith_shift_right, 13)
-    vw(n5)
-    v_t = tt(T.ot[:, :], T.t3[:, :], T.acc[:, :])
-    vw(n6)
     v_l = tt(T.ol[:, :], T.fa[:, :], T.fb[:, :])
-    S.wait_ge(sem.v, v_t)
-    S.dma_start(out=T.total[:], in_=T.ot[:, :]).then_inc(sem.outs, 16)
+    vw(n1)
+    v_t = tt(T.ot[:, :], T.t3[:, :], T.acc[:, :])
     Y.wait_ge(sem.v, v_l)
     Y.dma_start(out=T.last[:], in_=T.ol[:, :]).then_inc(sem.outs, 16)
+    S.wait_ge(sem.v, v_t)
+    S.dma_start(out=T.total[:], in_=T.ot[:, :]).then_inc(sem.outs, 16)
 
     for name in ("loc", "v", "s", "pe", "gi"):
         g.wait_ge(sem[name], cnt[name])

@@ -1,21 +1,22 @@
 from concourse.mybir import AluOpType as A, ActivationFunctionType as AF
 
-CAP = [3, 4, 5, 5]
-NS = [5, 4, 3, 3]
-N0 = [0, 5, 9, 12, 15]
+CAPS = [[3] * 5, [4] * 4, [5] * 3, [5] * 3]
 NV = 4
-BIG = 8388608.0
+NS = [len(c) for c in CAPS]
+N0 = [sum(NS[:t]) for t in range(NV + 1)]
+NN = N0[NV]
+BIG = 16777216.0
 SELU = 1048576.0
 
 SCRATCH = {"ps%d" % b: ("psum", [128, 32, 16], "float32") for b in range(8)}
 SCRATCH["srci"] = ("sbuf", [128, 4, 128], "int32")
 SCRATCH["s16"] = ("sbuf", [128, 128, 4], "float16")
 for _dt, _bufs in (
-        ("int32", "pidx 8 p31 8 p15 8 lst 144 lb 144 ei 64 hi 192 ha 192 fo 32 fin 32 fa 16 fb 16 t2 16 t3 16"),
+        ("int32", "pidx 8 p31 8 p15 8 lst 144 lq 144 ls 144 ei 64 hi 192 ha 192 fo 32 fin 32 fa 16 fb 16 t2 16 t3 16"),
         ("float16", "lr 512"),
         ("uint16", "l0 128 off 240 ho0 16 ho1 16 ho2 16 land1 16 land2 16 land3 16"),
-        ("float32", "ic 512 f31 8 f15 8 valc 8 row16 16 b16 16 sd 256 lt 144 lx 144 ls 144 xp 16 xq 16 ef 64"
-                    " le1 32 le2 32 le3 16 rr 240 uu 256 ad 256 ex 3840 sc 3840 gt 256 win 12288 wts 1024 tmp 2048"
+        ("float32", "ic 512 f31 8 f15 8 valc 8 row16 16 b16 16 sd 256 xp 16 xq 16 ef 64"
+                    " le1 32 le2 32 le3 16 rr 256 uu 256 ad 256 ex 3840 sc 3840 gt 256 win 12288 wts 1024 tmp 2048"
                     " vp1 64 vp2 48 hp 192 h96 96 h48 48 h16 16 acc 16 ol 16 ot 16")):
     _w = _bufs.split()
     for _i in range(0, len(_w), 2):
@@ -59,10 +60,10 @@ def rank_program(g, core, T, topo):
         return done("s", S.activation(out=out, in_=in_, func=func, bias=bias, scale=scale))
 
     Y.dma_start(out=T.srci[32:64, :, :], in_=T.nx[:]).then_inc(sem.lda, 16)
+    S.dma_start(out=T.srci[64:96, :, :], in_=T.w[:]).then_inc(sem.lda, 16)
     Y.dma_start(out=T.srci[0:32, :, :], in_=T.nx[:]).then_inc(sem.lda, 16)
-    Y.dma_start(out=T.srci[64:96, :, :], in_=T.w[:]).then_inc(sem.lda, 16)
     S.dma_start(out=T.ei[:, :], in_=T.e[:]).then_inc(sem.lde, 16)
-    S.dma_start(out=T.lst[:, 0:128], in_=T.nx[:]).then_inc(sem.ldb, 16)
+    Y.dma_start(out=T.lst[:, 0:128], in_=T.nx[:]).then_inc(sem.ldb, 16)
     S.dma_start(out=T.lst[:, 128:144], in_=T.x[:]).then_inc(sem.ldb, 16)
 
     g_p = done("gi", g.iota(T.pidx[:, 0:1], [[0, 1]], 0, 1))
@@ -70,11 +71,11 @@ def rank_program(g, core, T, topo):
     g_ic = done("gi", g.iota(T.ic[:, :], [[1, 4], [4, 8], [0, 16]], 0, 0, allow_small_or_imprecise_dtypes=True))
     g_id = done("gi", g.iota(T.win[:, 0:2048], [[512, 2048]], 0, 0, allow_small_or_imprecise_dtypes=True))
 
+    n = v(V.memset(T.sd[:, :], 0.0))
     v(V.memset(T.valc[0:32, 0:1], 8192.0))
     v(V.memset(T.valc[32:64, 0:1], -8188.0))
     v(V.memset(T.valc[64:96, 0:1], 1.0))
-    v(V.memset(T.ad[:, 240:256], 0.0))
-    n = v(V.memset(T.sd[:, :], 0.0))
+    v(V.memset(T.ad[:, 16 * NN:16 * NN + 16], 0.0))
     vw(n)
     v(V.memset(T.sd[:, 0:256:16], -BIG))
     V.wait_ge(sem.gi, g_p)
@@ -89,10 +90,10 @@ def rank_program(g, core, T, topo):
     V.wait_ge(sem.lde, 16)
     v_ef = vcopy(T.ef[:, :], T.ei[:, :])
     V.wait_ge(sem.lda, 48)
+    v_and = [ts(T.srci[32:64, :, c0:c0 + 64], T.srci[32:64, :, c0:c0 + 64], A.bitwise_and, 1920) for c0 in (0, 64)]
     v_half = []
     for c0 in (0, 64):
-        half = T.srci[32:64, :, c0:c0 + 64]
-        vw(ts(half, half, A.bitwise_and, 1920))
+        vw(v_and[c0 // 64])
         n = 0
         for i2 in range(4):
             n = vcopy(T.s16[0:96, c0:c0 + 64, i2], T.srci[0:96, i2, c0:c0 + 64])
@@ -128,15 +129,15 @@ def rank_program(g, core, T, topo):
         send(T["le%d" % t][:, :], T.ef[:, 16 * t:min(16 * t + 32, 64)], t, "ad%d" % t)
 
     def selectors(t, E):
-        m, k1 = CAP[t] * SELU, 1 if t else 0
+        m, k1 = CAPS[t][-1] * SELU, 1 if t else 0
         a, b = 16 * (N0[t] + k1), 16 * N0[t + 1]
         n = 0
         for k in range(k1, NS[t]):
             c = 16 * (N0[t] + k)
-            n = act(T.rr[:, c:c + 16], E[:, 0:16], AF.Relu, -m * k, SELU)
+            n = act(T.rr[:, c:c + 16], E[:, 0:16], AF.Relu, -SELU * sum(CAPS[t][:k]), SELU)
         m2, n2 = 0, 0
         if t < 3:
-            m2 = CAP[t + 1] * SELU
+            m2 = CAPS[t + 1][0] * SELU
             n2 = act(T.uu[:, b:b + 16], E[:, 16:32], AF.Relu, m2, -SELU)
         S.wait_ge(sem.s, n)
         n = act(T.uu[:, a:b], T.rr[:, a:b], AF.Relu, m, -1.0)
@@ -160,55 +161,55 @@ def rank_program(g, core, T, topo):
                          T.win[:, 2048 * (k - 1):2048 * k].indirect(T.l0[:, 32 * q:32 * q + 32]))
         return out
 
-    def add_w(k, pieces):
+    def add_w(k, pieces, which=(0, 1, 2, 3)):
         n = 0
-        for q in sorted(pieces):
-            V.wait_ge(sem.s, pieces[q])
-            c = 2048 * k + 512 * q
-            n = tt(T.win[:, c:c + 512], T.tmp[:, 512 * q:512 * q + 512], T["ps%d" % (4 + q)][:, :, :])
+        for q in which:
+            if q in pieces:
+                V.wait_ge(sem.s, pieces[q])
+                c = 2048 * k + 512 * q
+                n = tt(T.win[:, c:c + 512], T.tmp[:, 512 * q:512 * q + 512], T["ps%d" % (4 + q)][:, :, :])
         return n
 
-    def lower(k):
-        tt(T.win[:, 2048 * k:2048 * k + 1024], T.win[:, 2048 * (k - 1):2048 * k].indirect(T.l0[:, 0:64]), T.wts[:, :])
+    def lower(k, w=1024):
+        tt(T.win[:, 2048 * k:2048 * k + w], T.win[:, 2048 * (k - 1):2048 * k].indirect(T.l0[:, 0:w // 16]), T.wts[:, 0:w])
 
     S.wait_ge(sem.v, v_ef)
     s_ad = selectors(0, T.ef)
-    evac(1, False)
     S.wait_ge(sem.s, s_ad)
-    expand(0, 0, 3)
+    expand(0, 0, 5)
+    evac(1, False)
+    expand(0, 5, 8)
     s_r1 = evac(3, False)
 
     V.wait_ge(sem.ldb, 32)
-    n1 = ts(T.lb[:, :], T.lst[:, :], A.arith_shift_right, 7)
-    ts(T.lx[:, :], T.lst[:, :], A.mult, 16)
-    vw(n1)
-    vw(ts(T.lt[:, :], T.lb[:, :], A.mult, -2047))
-    vw(tt(T.ls[:, :], T.lt[:, :], T.lx[:, :]))
+    n = ts(T.lq[:, :], T.lst[:, :], A.mult, 2049)
+    evac(0, True)
+    vw(n)
+    vw(ts(T.ls[:, :], T.lq[:, :], A.arith_shift_right, 7, A.bitwise_and, 2047))
     vcopy(T.l0[:, :], T.ls[:, 0:128])
     n1 = ts(T.xp[:, :], T.ls[:, 128:144], A.mult, 512.0)
-    evac(0, True)
     v_r1 = evac(2, True)
     vw(n1)
     V.wait_ge(sem.s, s_ad)
     n1 = tt(T.xq[:, :], T.xp[:, :], T.ad[:, 0:16])
-    evac(4, True)
-    vw(n1)
-    ts(T.off[:, 0:16], T.xq[:, :], A.mult, 1.0 / 512)
-    v_w = evac(5, True)
+    v_w = evac(4, True)
 
     S.wait_ge(sem.v, v_r1)
     S.wait_ge(sem.s, s_r1)
-    part = raw(2, (2, 3))
-    expand(0, 3, 15)
+    part = raw(2, (1, 2, 3))
     vw(v_w)
     V.wait_ge(sem.s, s_r1)
-    lower(2)
+    lower(2, 512)
+    ts(T.off[:, 0:16], T.xq[:, :], A.mult, 1.0 / 512)
     V.wait_ge(sem.pe, 8)
-    n = add_w(2, part)
+    S.wait_ge(sem.v, add_w(2, part, (1,)))
+    s_w = evac(5, False)
+    n = add_w(2, part, (2, 3))
     S.wait_ge(sem.v, n)
     part = raw(3, (2, 3))
-    s_ex0 = expand(0, 15, 16)
+    s_ex0 = expand(0, 8, 16)
     vw(n)
+    V.wait_ge(sem.s, s_w)
     lower(3)
     n = add_w(3, part)
     vw(n)
@@ -222,30 +223,47 @@ def rank_program(g, core, T, topo):
     S.wait_ge(sem.v, n)
     part = raw(4, range(4))
     s_ex1 = visitors(1)
-    s_ex2 = visitors(2)
 
-    def res(j):
-        return T.sc[:, 256 * j + 15:256 * j + 256:16]
+    def res(j, a=0, b=256):
+        return T.sc[:, 256 * j + a + 15:256 * j + b:16]
 
     def visit(t, s_ready):
         V.wait_ge(sem.s, s_ready)
         if t:
             V.wait_ge(sem["hop%d" % t], landed(1))
         marks = []
+        last = [0, 0]
         for k in range(NS[t]):
             j = N0[t] + k
             off = T["land%d" % t][:, 0:16] if t and k == 0 else T.off[:, 16 * j:16 * j + 16]
+            ready = [0, 0]
             if k:
-                n = ts(off, res(j - 1), A.mult, 1.0 / 512)
-                if j == 14:
-                    tt(T.fo[:, 16:32], res(12), res(13))
-                vw(n)
-            vw(tt(T.gt[:, :], T.win[:, 0:2048 * (CAP[t] + 1)].indirect(off), T.ex[:, 256 * j:256 * j + 256]))
-            n = v(V.tensor_tensor_scan(out=T.sc[:, 256 * j:256 * j + 256], data0=T.sd[:, :], data1=T.gt[:, :],
-                                       initial=0.0, op0=A.add, op1=A.max))
-            vw(n)
-            marks.append(n)
+                for h in (0, 1):
+                    vw(last[h])
+                    ready[h] = ts(off[:, 8 * h:8 * h + 8] if t and k == 0 else T.off[:, 16 * j + 8 * h:16 * j + 8 * h + 8],
+                                  res(j - 1, 128 * h, 128 * h + 128), A.mult, 1.0 / 512)
+                if j == NN - 1:
+                    tt(T.fo[:, 16:32], res(j - 2), res(j - 1))
+            got = [0, 0]
+            for h in (0, 1):
+                if k:
+                    vw(ready[h])
+                    o = T.off[:, 16 * j + 8 * h:16 * j + 8 * h + 8]
+                elif t:
+                    o = T["land%d" % t][:, 8 * h:8 * h + 8]
+                else:
+                    o = T.off[:, 8 * h:8 * h + 8]
+                e0 = 256 * j + 128 * h
+                got[h] = tt(T.gt[:, 128 * h:128 * h + 128], T.win[:, 0:2048 * (CAPS[t][k] + 1)].indirect(o),
+                            T.ex[:, e0:e0 + 128])
+            for h in (0, 1):
+                vw(got[h])
+                e0 = 256 * j + 128 * h
+                last[h] = v(V.tensor_tensor_scan(out=T.sc[:, e0:e0 + 128], data0=T.sd[:, 0:128],
+                                                 data1=T.gt[:, 128 * h:128 * h + 128], initial=0.0, op0=A.add, op1=A.max))
+            marks.append(last[1])
         j = N0[t + 1] - 1
+        vw(last[1])
         if t < 3:
             return marks, ts(T["ho%d" % t][:, :], res(j), A.mult, 1.0 / 512)
         return marks, vcopy(T.fo[:, 0:16], res(j))
@@ -271,6 +289,7 @@ def rank_program(g, core, T, topo):
     vw(n)
     S.wait_ge(sem.v, n)
     part = raw(5, range(4))
+    s_ex2 = visitors(2)
     s_own = keep(0, marks, T.hp)
 
     marks, n = visit(1, s_ex1)

@@ -1,27 +1,35 @@
 from concourse.mybir import AluOpType as A, ActivationFunctionType as AF
 
-CAPS = [[3] * 5, [4] * 4, [5] * 3, [5] * 3]
 NV = 4
-NS = [len(c) for c in CAPS]
-N0 = [sum(NS[:t]) for t in range(NV + 1)]
-NN = N0[NV]
 BIG = 16777216.0
-SELU = 1048576.0
+FAR = 32768.0
 
-SCRATCH = {"ps%d" % b: ("psum", [128, 32, 16], "float32") for b in range(8)}
+SCRATCH = {"ps%d" % b: ("psum", [128, 32, 16] if b < 4 else [128, 512], "float32") for b in range(8)}
 SCRATCH["srci"] = ("sbuf", [128, 4, 128], "int32")
 SCRATCH["s16"] = ("sbuf", [128, 128, 4], "float16")
+SCRATCH["jj"] = ("sbuf", [128, 128, 4], "float32")
+SCRATCH["lr"] = ("sbuf", [128, 32, 16], "float16")
+SCRATCH["ic"] = ("sbuf", [128, 32, 16], "float32")
+SCRATCH["dl"] = ("sbuf", [128, 8, 16], "float32")
+SCRATCH["kk"] = ("sbuf", [128, 8, 16], "float32")
+for _m in (1, 2, 4):
+    SCRATCH["sh%d" % _m] = ("sbuf", [128, 8, 16], "float16")
 for _dt, _bufs in (
-        ("int32", "pidx 8 p31 8 p15 8 lst 144 lq 144 ls 144 ei 64 hi 192 ha 192 fo 32 fin 32 fa 16 fb 16 t2 16 t3 16"),
-        ("float16", "lr 512"),
-        ("uint16", "l0 128 off 240 ho0 16 ho1 16 ho2 16 land1 16 land2 16 land3 16"),
-        ("float32", "ic 512 f31 8 f15 8 valc 8 row16 16 b16 16 sd 256 xp 16 xq 16 ef 64"
-                    " le1 32 le2 32 le3 16 rr 256 uu 256 ad 256 ex 3840 sc 3840 gt 256 win 12288 wts 1024 tmp 2048"
-                    " vp1 64 vp2 48 hp 192 h96 96 h48 48 h16 16 acc 16 ol 16 ot 16")):
+        ("int32", "pidx 8 pq 8 p3 8 p31 8 p15 8 lst 144 lq 144 ls 144 ei 64 fo 16 fin 16 fa 16 fb 16 t3 16 w0 2048"),
+        ("float16", "y1 144 y2 144 y4 144 sums 128 sumw 128 sumf 128"
+                    " g1 2048 g2 2048 g3 2048 mm0 256 mm1 256 mm2 256 mm3 256 mw0 256"),
+        ("bfloat16", "idb 128 idf 128 far 256 hx0 256 hx1 256 hx2 256"),
+        ("uint16", "l1 128 l2 128 l4 128 l8 128 eu 64 le1 32 le2 32 le3 16 off0 16 ho0 16 ho1 16 ho2 16"
+                   " land1 16 land2 16 land3 16"),
+        ("float32", "f31 8 f15 8 i8 8 f4 8 isl 8 nis 8 sg 8 valc 8 gcol 8 ge8 8 lt8 8 sf 8 c7 8 cn 8 c15 8"
+                    " ay1 144 ay2 144 ay4 144 xk 144 em 16 eh 16 ht 16 mta 16 mtb 16 mt 16 g16 128 l256 256"
+                    " hi0 16 xo 16"
+                    " sd 256 ta 2048 tb 2048 win 4096 mk0 256 mk1 256 mk2 256 mk3 256 sc 256 sw 256 gw 256"
+                    " wl0 16 wl1 16 wl2 16 wr1 16 wr2 16 acc1 16 acc 16 ol 16 ot 16")):
     _w = _bufs.split()
     for _i in range(0, len(_w), 2):
         SCRATCH[_w[_i]] = ("sbuf", [128, int(_w[_i + 1])], _dt)
-SEMAPHORES = ["v", "s", "pe", "gi", "lda", "ldb", "lde", "outs", "loc",
+SEMAPHORES = ["v", "s", "pe", "gi", "lda", "ldb", "lde", "lw", "cp", "outs", "loc",
               "ad1", "ad2", "ad3", "hop1", "hop2", "hop3", "hop4", "bg1", "bg2"]
 
 
@@ -39,81 +47,140 @@ def rank_program(g, core, T, topo):
         cnt[name] += 1
         return cnt[name]
 
-    def v(ins):
-        return done("v", ins)
-
     def vw(n):
         V.wait_ge(sem.v, n)
 
     def ts(out, in0, op, c, op1=None, c1=None):
         if op1 is None:
-            return v(V.tensor_scalar(out=out, in0=in0, scalar1=c, scalar2=None, op0=op))
-        return v(V.tensor_scalar(out=out, in0=in0, scalar1=c, scalar2=c1, op0=op, op1=op1))
+            return done("v", V.tensor_scalar(out=out, in0=in0, scalar1=c, scalar2=None, op0=op))
+        return done("v", V.tensor_scalar(out=out, in0=in0, scalar1=c, scalar2=c1, op0=op, op1=op1))
 
     def tt(out, in0, in1, op=A.add):
-        return v(V.tensor_tensor(out=out, in0=in0, in1=in1, op=op))
+        return done("v", V.tensor_tensor(out=out, in0=in0, in1=in1, op=op))
 
     def vcopy(out, in_):
-        return v(V.tensor_copy(out=out, in_=in_))
+        return done("v", V.tensor_copy(out=out, in_=in_))
+
+    def fill(ap, c):
+        return done("v", V.memset(ap, c))
 
     def act(out, in_, func=AF.Copy, bias=0.0, scale=1.0):
         return done("s", S.activation(out=out, in_=in_, func=func, bias=bias, scale=scale))
 
+    def mm(out, lhsT, rhs, start, stop, count=True):
+        ins = PE.matmul(out=out, lhsT=lhsT, rhs=rhs, start=start, stop=stop)
+        return done("pe", ins) if count else 0
+
+    Y.dma_start(out=T.lst[:, 0:128], in_=T.nx[:]).then_inc(sem.ldb, 16)
+    S.dma_start(out=T.lst[:, 128:144], in_=T.x[:]).then_inc(sem.ldb, 16)
     Y.dma_start(out=T.srci[32:64, :, :], in_=T.nx[:]).then_inc(sem.lda, 16)
     S.dma_start(out=T.srci[64:96, :, :], in_=T.w[:]).then_inc(sem.lda, 16)
     Y.dma_start(out=T.srci[0:32, :, :], in_=T.nx[:]).then_inc(sem.lda, 16)
     S.dma_start(out=T.ei[:, :], in_=T.e[:]).then_inc(sem.lde, 16)
-    Y.dma_start(out=T.lst[:, 0:128], in_=T.nx[:]).then_inc(sem.ldb, 16)
-    S.dma_start(out=T.lst[:, 128:144], in_=T.x[:]).then_inc(sem.ldb, 16)
+
+    def iota(ap, pattern, cm=0, base=0):
+        return done("gi", g.iota(ap, pattern, base, cm, allow_small_or_imprecise_dtypes=True))
 
     g_p = done("gi", g.iota(T.pidx[:, 0:1], [[0, 1]], 0, 1))
-    done("gi", g.iota(T.row16[:, :], [[1, 16]], 0, 0, allow_small_or_imprecise_dtypes=True))
-    g_ic = done("gi", g.iota(T.ic[:, :], [[1, 4], [4, 8], [0, 16]], 0, 0, allow_small_or_imprecise_dtypes=True))
-    g_id = done("gi", g.iota(T.win[:, 0:2048], [[512, 2048]], 0, 0, allow_small_or_imprecise_dtypes=True))
+    g_i = iota(T.i8[:, :], [[1, 8]])
+    g_0 = done("gi", g.iota(T.w0[:, 512:1024], [[0, 512]], 0, 0))
+    g_c = iota(T.ic[:, :, :], [[1, 4], [4, 8], [0, 16]])
+    g_x = iota(T.xk[:, :], [[1, 144]], -1)
+    iota(T.dl[:, :, :], [[16, 8], [1, 16]], -1)
+    g_k = iota(T.kk[:, :, :], [[-16, 8], [0, 16]], 1)
+    g_q = done("gi", g.iota(T.pq[:, 0:1], [[0, 1]], 0, 4))
+    g_j = iota(T.jj[:, :, :], [[16, 128], [1, 4]])
+    iota(T.em[:, :], [[0, 2], [1, 8]])
+    iota(T.eh[:, :], [[1, 2], [0, 8]])
+    iota(T.ht[:, :], [[2048, 2], [0, 8]])
+    iota(T.g16[:, :], [[16, 8], [0, 16]])
+    iota(T.l256[:, :], [[0, 16], [1, 16]])
+    g_l = iota(T.sd[:, :], [[0, 256]])
 
-    n = v(V.memset(T.sd[:, :], 0.0))
-    v(V.memset(T.valc[0:32, 0:1], 8192.0))
-    v(V.memset(T.valc[32:64, 0:1], -8188.0))
-    v(V.memset(T.valc[64:96, 0:1], 1.0))
-    v(V.memset(T.ad[:, 16 * NN:16 * NN + 16], 0.0))
-    vw(n)
-    v(V.memset(T.sd[:, 0:256:16], -BIG))
+    n = fill(T.w0[:, 0:512], 0)
+    S.wait_ge(sem.v, n)
+    for q in (2, 3):
+        s_0 = act(T.w0[:, 512 * q:512 * q + 512], T.w0[:, 0:512])
+    Y.wait_ge(sem.v, n)
+    Y.wait_ge(sem.s, s_0)
+    Y.wait_ge(sem.gi, g_0)
+    Y.dma_start(out=T.w0[8:128:16, :], in_=T.w[:]).then_inc(sem.lw, 16)
+    S.wait_ge(sem.ldb, 32)
+    for i in range(0, 32, 8):
+        s_lr = act(T.lr[:, i:i + 8, :], T.lst[:, 0:128], AF.Copy, 0.0, 0.0)
+    fill(T.valc[0:32, 0:1], 16.0)
+    fill(T.valc[32:64, 0:1], -2047.0 / 128)
     V.wait_ge(sem.gi, g_p)
-    ts(T.p31[:, 0:1], T.pidx[:, 0:1], A.bitwise_and, 31)
-    vw(ts(T.p15[:, 0:1], T.pidx[:, 0:1], A.bitwise_and, 15))
+    n1 = ts(T.p31[:, 0:1], T.pidx[:, 0:1], A.bitwise_and, 31)
+    n2 = ts(T.p15[:, 0:1], T.pidx[:, 0:1], A.bitwise_and, 15)
+    vw(n1)
     vcopy(T.f31[:, 0:1], T.p31[:, 0:1])
-    vw(vcopy(T.f15[:, 0:1], T.p15[:, 0:1]))
-    V.wait_ge(sem.gi, g_ic)
-    ts(T.b16[:, :], T.row16[:, :], A.not_equal, T.f15[:, 0:1], A.mult, -BIG)
-    ts(T.lr[0:96, :], T.ic[0:96, :], A.is_equal, T.f31[0:96, 0:1], A.mult, T.valc[0:96, 0:1])
+    vw(n2)
+    n2 = vcopy(T.f15[:, 0:1], T.p15[:, 0:1])
 
-    V.wait_ge(sem.lde, 16)
-    v_ef = vcopy(T.ef[:, :], T.ei[:, :])
+    V.wait_ge(sem.ldb, 32)
+    n = ts(T.lq[:, :], T.lst[:, :], A.mult, 2049)
+    v_l = vcopy(T.l1[:, :], T.lst[:, 0:128])
+    vw(n)
+    v_c = ts(T.ls[:, :], T.lq[:, :], A.arith_shift_right, 7, A.bitwise_and, 2047)
+    Y.wait_ge(sem.v, v_c)
+    Y.dma_start(out=T.w0[1:128:16, :], in_=T.ls[:, 0:128]).then_inc(sem.lw, 16)
+
     V.wait_ge(sem.lda, 48)
-    v_and = [ts(T.srci[32:64, :, c0:c0 + 64], T.srci[32:64, :, c0:c0 + 64], A.bitwise_and, 1920) for c0 in (0, 64)]
-    v_half = []
     for c0 in (0, 64):
-        vw(v_and[c0 // 64])
-        n = 0
-        for i2 in range(4):
-            n = vcopy(T.s16[0:96, c0:c0 + 64, i2], T.srci[0:96, i2, c0:c0 + 64])
-        v_half.append(n)
+        n = ts(T.srci[32:64, :, c0:c0 + 64], T.srci[32:64, :, c0:c0 + 64], A.bitwise_and, 1920)
+        S.wait_ge(sem.v, n)
+        for i2 in (2, 3):
+            s_16 = act(T.s16[0:96, c0:c0 + 64, i2], T.srci[0:96, i2, c0:c0 + 64])
+    v_and = n
+    V.wait_ge(sem.gi, g_i)
+    v_is = ts(T.isl[:, :], T.i8[:, :], A.is_equal, T.f15[:, 0:1])
+    V.wait_ge(sem.gi, g_c)
+    V.wait_ge(sem.s, s_lr)
+    ts(T.lr[64:96, :, 8:16], T.ic[64:96, :, 8:16], A.is_equal, T.f31[64:96, 0:1])
+    ts(T.lr[96:128, :, 0:1], T.ic[96:128, :, 0:1], A.is_equal, T.f31[96:128, 0:1])
+    ts(T.lr[0:64, :, 1:2], T.ic[0:64, :, 1:2], A.is_equal, T.f31[0:64, 0:1], A.mult, T.valc[0:64, 0:1])
+    vw(v_and)
+    for i2 in (0, 1):
+        v_16 = vcopy(T.s16[0:96, :, i2], T.srci[0:96, i2, :])
 
-    for bank in range(8):
-        c0 = 32 * (bank % 4)
-        k0 = 0 if bank < 4 else 64
-        if bank in (0, 2):
-            PE.wait_ge(sem.v, v_half[bank // 2])
+    s_sh = {}
+    s_y = {}
+
+    def zero(m):
+        s_sh[m] = act(T["sh%d" % m][:, :, :], T.lst[:, 0:128], AF.Copy, 0.0, 0.0)
+
+    def diag(m):
+        n = act(T["ay%d" % m][:, :], T.xk[:, :], AF.Abs, m - 15.0)
+        S.wait_ge(sem.s, n)
+        s_y[m] = act(T["y%d" % m][:, :], T["ay%d" % m][:, :], AF.Relu, T.isl[:, m:m + 1], T.nis[:, m:m + 1])
+
+    zero(1)
+    zero(2)
+    S.wait_ge(sem.v, v_is)
+    nis = act(T.nis[:, :], T.isl[:, :], AF.Copy, 0.0, -1.0)
+
+    def shifts(m):
+        sh = T["sh%d" % m]
+        V.wait_ge(sem.s, s_sh[m])
+        n = ts(sh[:, :, m + 1:min(2 * m + 1, 8)], T.dl[:, :, m + 1:min(2 * m + 1, 8)], A.is_equal, float(m))
+        k = 8 + 2 * m if m > 1 else 9
+        if m > 1:
+            n = ts(sh[:, :, 8 + m:k], T.dl[:, :, 8 + m:k], A.is_equal, float(m))
+        if m < 4:
+            n = ts(sh[:, :, k:16], T.kk[:, :, k:16], A.is_equal, 7.0 + m)
+        return n
+
+    v_sh = {}
+
+    ps = [T["ps%d" % b] for b in range(8)]
+    full = lambda q: ps[q][:, :, :]
+    cols = lambda t, q: t[:, 512 * q:512 * q + 512]
+
+    def first(q, k0, k1):
         for h in range(4):
-            ins = PE.matmul(out=T["ps%d" % bank][:, :, 4 * h:4 * h + 4], lhsT=T.lr[k0:96, 128 * h:128 * h + 128],
-                            rhs=T.s16[k0:96, c0:c0 + 32, :], start=True, stop=True)
-        done("pe", ins)
-
-    def evac(bank, on_vector):
-        (V if on_vector else S).wait_ge(sem.pe, bank + 1)
-        q0 = 512 * (bank % 4)
-        out = T.win[:, 2048 + q0:2560 + q0] if bank < 4 else T.wts[:, q0:q0 + 512]
-        return (vcopy if on_vector else act)(out, T["ps%d" % bank][:, :, :])
+            mm(ps[q][:, :, 4 * h:4 * h + 4], T.lr[k0:k1, 8 * h:8 * h + 8, :], T.s16[k0:k1, 32 * q:32 * q + 32, :],
+               h == 0, False, False)
 
     def send(out, src, d, name):
         dst = peer(d)
@@ -124,210 +191,251 @@ def rank_program(g, core, T, topo):
     def landed(d):
         return len(topo.engines(peer(-d), core))
 
-    g.wait_ge(sem.v, v_ef)
-    for t in (1, 2, 3):
-        send(T["le%d" % t][:, :], T.ef[:, 16 * t:min(16 * t + 32, 64)], t, "ad%d" % t)
+    v_at = {}
+    s_at = {}
 
-    def selectors(t, E):
-        m, k1 = CAPS[t][-1] * SELU, 1 if t else 0
-        a, b = 16 * (N0[t] + k1), 16 * N0[t + 1]
-        n = 0
-        for k in range(k1, NS[t]):
-            c = 16 * (N0[t] + k)
-            n = act(T.rr[:, c:c + 16], E[:, 0:16], AF.Relu, -SELU * sum(CAPS[t][:k]), SELU)
-        m2, n2 = 0, 0
-        if t < 3:
-            m2 = CAPS[t + 1][0] * SELU
-            n2 = act(T.uu[:, b:b + 16], E[:, 16:32], AF.Relu, m2, -SELU)
-        S.wait_ge(sem.s, n)
-        n = act(T.uu[:, a:b], T.rr[:, a:b], AF.Relu, m, -1.0)
-        if t < 3:
-            S.wait_ge(sem.s, n2)
-            act(T.ad[:, b:b + 16], T.uu[:, b:b + 16], AF.Identity, m2, -1.0)
-        S.wait_ge(sem.s, n)
-        return act(T.ad[:, a:b], T.uu[:, a:b], AF.Identity, m, -1.0)
+    def vector_extra(m):
+        if m == 1:
+            V.wait_ge(sem.gi, g_q)
+            n = ts(T.p3[:, 0:1], T.pq[:, 0:1], A.bitwise_and, 12)
+            V.wait_ge(sem.lde, 16)
+            v_at["eu"] = vcopy(T.eu[:, :], T.ei[:, :])
+            vw(n)
+            v_at["f4"] = vcopy(T.f4[:, 0:1], T.p3[:, 0:1])
+            v_sh[2] = shifts(2)
+        elif m == 2:
+            n = ts(T.hi0[:, :], T.ei[:, 0:16], A.is_ge, 8, A.mult, 2048.0)
+            tt(T.gcol[:, 0:1], T.pidx[:, 0:1], T.p15[:, 0:1], A.subtract)
+            v_sh[4] = shifts(4)
+            vw(n)
+            n = tt(T.xo[:, :], T.ls[:, 128:144], T.hi0[:, :])
+            ts(T.idb[:, :], T.dl[:, :, :], A.is_equal, 0.0)
+            vw(n)
+            vcopy(T.off0[:, :], T.xo[:, :])
+        else:
+            V.wait_ge(sem.gi, g_l)
+            V.wait_ge(sem.s, s_at["lt8"])
+            ts(T.mta[:, :], T.em[:, :], A.is_equal, T.cn[:, 0:1])
+            n = ts(T.mtb[:, :], T.eh[:, :], A.mult, T.c15[:, 0:1])
+            fill(T.sd[:, 0:256:16], -BIG)
+            vw(n)
+            v_at["mt"] = tt(T.mt[:, :], T.mta[:, :], T.mtb[:, :])
+            ts(T.sums[:, :], T.g16[:, :], A.is_equal, T.gcol[:, 0:1], A.mult, T.lt8[:, 0:1])
+            v_at["far"] = ts(T.far[:, :], T.l256[:, :], A.not_equal, T.f15[:, 0:1], A.mult, -FAR)
 
-    def expand(t, i0, i1):
-        n = 0
-        for i in range(i0, i1):
-            n = act(T.ex[:, 256 * N0[t] + i:256 * N0[t + 1]:16], T.ad[:, 16 * N0[t] + 16:16 * N0[t + 1] + 16], AF.Identity,
-                    T.b16[:, i:i + 1])
-        return n
+    def scalar_extra(m):
+        if m == 1:
+            diag(2)
+            zero(4)
+            S.wait_ge(sem.gi, g_j)
+            S.wait_ge(sem.v, v_at["f4"])
+            s_at["id"] = act(T.s16[96:128, :, :], T.jj[96:128, :, :], AF.Identity, T.f4[96:128, 0:1])
+        elif m == 2:
+            diag(4)
+            n = act(T.sg[:, 0:1], T.f15[:, 0:1], AF.Sign, -7.5)
+            act(T.c15[:, 0:1], T.f15[:, 0:1], AF.Relu, -14.0)
+            S.wait_ge(sem.s, n)
+            n = act(T.c7[:, 0:1], T.sg[:, 0:1], AF.Copy, -3.5, -3.5)
+            S.wait_ge(sem.s, n)
+            act(T.cn[:, 0:1], T.f15[:, 0:1], AF.Identity, T.c7[:, 0:1])
+            s_at["lt8"] = act(T.lt8[:, 0:1], T.sg[:, 0:1], AF.Copy, 0.5, -0.5)
+        else:
+            S.wait_ge(sem.v, v_at["mt"])
+            act(T.mk0[:, :], T.mt[:, :].indirect(T.eu[:, 0:16]))
 
-    def raw(k, pieces):
-        out = {}
-        for q in pieces:
-            out[q] = act(T.tmp[:, 512 * q:512 * q + 512],
-                         T.win[:, 2048 * (k - 1):2048 * k].indirect(T.l0[:, 32 * q:32 * q + 32]))
-        return out
+    tabs = {1: (T.w0, T.tb), 2: (T.tb, T.ta), 4: (T.ta, T.win)}
+    lists = {1: T.l1, 2: T.l2, 4: T.l4, 8: T.l8}
+    gs = {1: T.g1, 2: T.g2, 4: T.g3}
+    v_l = {1: v_l, 0: v_l}
+    v_ev, s_ev = v_l[0], s_0
+    for m in (1, 2, 4):
+        old, new = tabs[m]
+        G, L, Ln, sh = gs[m], lists[m], lists[2 * m], T["sh%d" % m]
+        ind = lambda q: old[:, 0:2048].indirect(L[:, 32 * q:32 * q + 32])
+        if m == 1:
+            V.wait_ge(sem.lw, 32)
+            S.wait_ge(sem.lw, 32)
+        vw(max(v_ev, v_l[0]))
+        V.wait_ge(sem.s, s_ev)
+        vg = {0: vcopy(cols(G, 0), ind(0))}
+        if m == 1:
+            V.wait_ge(sem.gi, g_k)
+            v_sh[1] = shifts(1)
+        vg[1] = vcopy(cols(G, 1), ind(1))
+        S.wait_ge(sem.v, max(v_ev, v_l[1]))
+        S.wait_ge(sem.s, s_ev)
+        sg = {q: act(cols(G, q), ind(q)) for q in (2, 3)}
+        if m == 1:
+            S.wait_ge(sem.gi, g_x)
+            S.wait_ge(sem.s, nis)
+            diag(1)
 
-    def add_w(k, pieces, which=(0, 1, 2, 3)):
-        n = 0
-        for q in which:
-            if q in pieces:
-                V.wait_ge(sem.s, pieces[q])
-                c = 2048 * k + 512 * q
-                n = tt(T.win[:, c:c + 512], T.tmp[:, 512 * q:512 * q + 512], T["ps%d" % (4 + q)][:, :, :])
-        return n
+        if m == 1:
+            PE.wait_ge(sem.v, v_16)
+            PE.wait_ge(sem.s, s_16)
+            for q in range(4):
+                first(q, 0, 96)
+            PE.wait_ge(sem.v, v_sh[1])
+        else:
+            PE.wait_ge(sem.v, max(v_ev, v_sh[m]))
+            PE.wait_ge(sem.s, s_ev)
+            for q in (2, 3):
+                first(q, 0, 96 if m == 2 else 128)
+                mm(full(q), T.sh1[:, :, :], cols(T.g1, q), False, False, False)
+                if m > 2:
+                    mm(full(q), T.sh2[:, :, :], cols(T.g2, q), False, False, False)
+            if m == 2:
+                PE.wait_ge(sem.s, s_at["id"])
+                for q in (0, 1):
+                    first(q, 96, 128)
 
-    def lower(k, w=1024):
-        tt(T.win[:, 2048 * k:2048 * k + w], T.win[:, 2048 * (k - 1):2048 * k].indirect(T.l0[:, 0:w // 16]), T.wts[:, 0:w])
+        def extract(half):
+            n = 0
+            for b in range(16):
+                n = mm(ps[4 + half][:, 0:64], T["y%d" % m][:, 15 - b:143 - b],
+                       G[:, 1024 * half + b:1024 * half + 1024:16], b == 0, b == 15, b == 15)
+            return n
 
-    S.wait_ge(sem.v, v_ef)
-    s_ad = selectors(0, T.ef)
-    S.wait_ge(sem.s, s_ad)
-    expand(0, 0, 5)
-    evac(1, False)
-    expand(0, 5, 8)
-    s_r1 = evac(3, False)
+        pc = {}
+        for q in (0, 2, 1, 3):
+            if q < 2:
+                PE.wait_ge(sem.v, vg[q])
+            else:
+                PE.wait_ge(sem.s, sg[q])
+            pc[q] = mm(full(q), sh[:, :, :], cols(G, q), q < 2 and m == 4, True)
+        PE.wait_ge(sem.s, s_y[m])
+        px = {h: extract(h) for h in (1, 0)}
+        for q in (2, 3):
+            S.wait_ge(sem.pe, pc[q])
+            s_ev = act(cols(new, q), full(q))
+        for q in (0, 1):
+            V.wait_ge(sem.pe, pc[q])
+            v_ev = tt(cols(new, q), cols(old, q), full(q)) if m > 1 else vcopy(cols(new, q), full(q))
+        vector_extra(m)
+        scalar_extra(m)
+        for h in (1, 0):
+            V.wait_ge(sem.pe, px[h])
+            v_l[h] = vcopy(Ln[:, 64 * h:64 * h + 64], ps[4 + h][:, 0:64])
+        if m == 1:
+            g.wait_ge(sem.v, v_at["eu"])
+            for t in (1, 2, 3):
+                send(T["le%d" % t][:, :], T.eu[:, 16 * t:min(16 * t + 32, 64)], t, "ad%d" % t)
 
-    V.wait_ge(sem.ldb, 32)
-    n = ts(T.lq[:, :], T.lst[:, :], A.mult, 2049)
-    evac(0, True)
-    vw(n)
-    vw(ts(T.ls[:, :], T.lq[:, :], A.arith_shift_right, 7, A.bitwise_and, 2047))
-    vcopy(T.l0[:, :], T.ls[:, 0:128])
-    n1 = ts(T.xp[:, :], T.ls[:, 128:144], A.mult, 512.0)
-    v_r1 = evac(2, True)
-    vw(n1)
-    V.wait_ge(sem.s, s_ad)
-    n1 = tt(T.xq[:, :], T.xp[:, :], T.ad[:, 0:16])
-    v_w = evac(4, True)
-
-    S.wait_ge(sem.v, v_r1)
-    S.wait_ge(sem.s, s_r1)
-    part = raw(2, (1, 2, 3))
-    vw(v_w)
-    V.wait_ge(sem.s, s_r1)
-    lower(2, 512)
-    ts(T.off[:, 0:16], T.xq[:, :], A.mult, 1.0 / 512)
-    V.wait_ge(sem.pe, 8)
-    S.wait_ge(sem.v, add_w(2, part, (1,)))
-    s_w = evac(5, False)
-    n = add_w(2, part, (2, 3))
-    S.wait_ge(sem.v, n)
-    part = raw(3, (2, 3))
-    s_ex0 = expand(0, 8, 16)
+    win = T.win[:, 0:4096]
+    ind = lambda q: T.win[:, 0:2048].indirect(T.l8[:, 32 * q:32 * q + 32])
+    vw(v_l[0])
+    V.wait_ge(sem.s, s_ev)
+    for q in (0, 1):
+        n = vcopy(cols(T.win, 4 + q), ind(q))
+    S.wait_ge(sem.v, v_l[1])
+    S.wait_ge(sem.s, s_ev)
+    for q in (2, 3):
+        s_w = act(cols(T.win, 4 + q), ind(q))
     vw(n)
     V.wait_ge(sem.s, s_w)
-    lower(3)
-    n = add_w(3, part)
-    vw(n)
-    V.wait_ge(sem.gi, g_id)
 
-    def visitors(t):
+    s_at[0] = act(T.hx0[:, :], T.ht[:, :].indirect(T.eu[:, 16:32]))
+    act(T.ge8[:, 0:1], T.sg[:, 0:1], AF.Copy, 0.5, 0.5)
+    s_at["sf"] = act(T.sf[:, 0:1], T.sg[:, 0:1], AF.Copy, 256.5, -255.5)
+    for t in (1, 2, 3):
         S.wait_ge(sem["ad%d" % t], landed(t))
-        S.wait_ge(sem.s, selectors(t, T["le%d" % t]))
-        return expand(t, 0, 16)
+        le = T["le%d" % t]
+        s_at[t] = act(T["mk%d" % t][:, :], T.mt[:, :].indirect(le[:, 0:16]))
+        if t < 3:
+            s_at[t] = act(T["hx%d" % t][:, :], T.ht[:, :].indirect(le[:, 16:32]))
 
-    S.wait_ge(sem.v, n)
-    part = raw(4, range(4))
-    s_ex1 = visitors(1)
-
-    def res(j, a=0, b=256):
-        return T.sc[:, 256 * j + a + 15:256 * j + b:16]
-
-    def visit(t, s_ready):
-        V.wait_ge(sem.s, s_ready)
+    def visit(t, v_free):
+        off = T["land%d" % t] if t else T.off0
+        M, mk = T["mm%d" % t], T["mk%d" % t]
+        if t:
+            V.wait_ge(sem.s, s_at[t])
+        if t == 1:
+            V.wait_ge(sem.cp, 16)
         if t:
             V.wait_ge(sem["hop%d" % t], landed(1))
-        marks = []
-        last = [0, 0]
-        for k in range(NS[t]):
-            j = N0[t] + k
-            off = T["land%d" % t][:, 0:16] if t and k == 0 else T.off[:, 16 * j:16 * j + 16]
-            ready = [0, 0]
-            if k:
-                for h in (0, 1):
-                    vw(last[h])
-                    ready[h] = ts(off[:, 8 * h:8 * h + 8] if t and k == 0 else T.off[:, 16 * j + 8 * h:16 * j + 8 * h + 8],
-                                  res(j - 1, 128 * h, 128 * h + 128), A.mult, 1.0 / 512)
-                if j == NN - 1:
-                    tt(T.fo[:, 16:32], res(j - 2), res(j - 1))
-            got = [0, 0]
-            for h in (0, 1):
-                if k:
-                    vw(ready[h])
-                    o = T.off[:, 16 * j + 8 * h:16 * j + 8 * h + 8]
-                elif t:
-                    o = T["land%d" % t][:, 8 * h:8 * h + 8]
-                else:
-                    o = T.off[:, 8 * h:8 * h + 8]
-                e0 = 256 * j + 128 * h
-                got[h] = tt(T.gt[:, 128 * h:128 * h + 128], T.win[:, 0:2048 * (CAPS[t][k] + 1)].indirect(o),
-                            T.ex[:, e0:e0 + 128])
-            for h in (0, 1):
-                vw(got[h])
-                e0 = 256 * j + 128 * h
-                last[h] = v(V.tensor_tensor_scan(out=T.sc[:, e0:e0 + 128], data0=T.sd[:, 0:128],
-                                                 data1=T.gt[:, 128 * h:128 * h + 128], initial=0.0, op0=A.add, op1=A.max))
-            marks.append(last[1])
-        j = N0[t + 1] - 1
-        vw(last[1])
+        vg = [tt(M[:, 128 * h:128 * h + 128], win.indirect(off[:, 8 * h:8 * h + 8]), mk[:, 128 * h:128 * h + 128], A.mult)
+              for h in (0, 1)]
+        PE.wait_ge(sem.v, max(v_free, v_at["far"]) if t < 3 else max(v_free, v_at["sumf"]))
         if t < 3:
-            return marks, ts(T["ho%d" % t][:, :], res(j), A.mult, 1.0 / 512)
-        return marks, vcopy(T.fo[:, 0:16], res(j))
+            PE.wait_ge(sem.s, s_at[t])
+        for h in (0, 1):
+            mm(ps[6 + h][:, 0:128], (T.idb if t < 3 else T.idf)[:, :], T.far[:, 0:128], True, False, False)
+            if t < 3:
+                mm(ps[6 + h][:, 0:128], T.idb[:, :], T["hx%d" % t][:, 128 * h:128 * h + 128], False, False, False)
+        pr = []
+        for h in (0, 1):
+            PE.wait_ge(sem.v, vg[h])
+            pr.append(mm(ps[6 + h][:, 0:128], (T.sums if t < 3 else T.sumf)[:, :], M[:, 128 * h:128 * h + 128],
+                         False, True))
+        for h in (0, 1):
+            V.wait_ge(sem.pe, pr[h])
+            n = done("v", V.tensor_tensor_scan(out=T.sc[:, 128 * h:128 * h + 128], data0=T.sd[:, 0:128],
+                                               data1=ps[6 + h][:, 0:128], initial=0.0, op0=A.add, op1=A.max))
+        vw(n)
+        out = T["ho%d" % t] if t < 3 else T.fo
+        return vg[1], n, vcopy(out[:, :], T.sc[:, 15:256:16])
 
     def hand_on(t, n):
         g.wait_ge(sem.v, n)
         send(T["land%d" % (t + 1)][:, :], T["ho%d" % t][:, :], 1, "hop%d" % (t + 1))
 
-    def keep(t, marks, H):
-        n = 0
-        for k, mark in enumerate(marks):
-            S.wait_ge(sem.v, mark)
-            n = act(H[:, 16 * k:16 * k + 16], res(N0[t] + k))
-        return n
+    def weights(t, M, n, v_free):
+        PE.wait_ge(sem.v, max(n, v_free))
+        mm(ps[4][:, 0:256], T.idb[:, :], T.far[:, :], True, False, False)
+        p = mm(ps[4][:, 0:256], T.sumw[:, :], M[:, :], False, True)
+        V.wait_ge(sem.pe, p)
+        n = done("v", V.tensor_tensor_scan(out=T.sw[:, :], data0=T.sd[:, :], data1=ps[4][:, 0:256],
+                                           initial=0.0, op0=A.add, op1=A.max))
+        vw(n)
+        return n, vcopy(T["wl%d" % t][:, :], T.sw[:, 15:256:16])
 
     def report(t, n):
-        g.wait_ge(sem.s, n)
-        send(T.hp[:, 16 * N0[t]:16 * N0[t + 1]], T["vp%d" % t][:, :], -t, "bg%d" % t)
+        g.wait_ge(sem.v, n)
+        send(T["wr%d" % t][:, :], T["wl%d" % t][:, :], -t, "bg%d" % t)
 
-    marks, n = visit(0, s_ex0)
+    vg, v_sc, n = visit(0, max(v_l.values()))
     hand_on(0, n)
-    n = add_w(4, part)
-    vw(n)
-    S.wait_ge(sem.v, n)
-    part = raw(5, range(4))
-    s_ex2 = visitors(2)
-    s_own = keep(0, marks, T.hp)
+    Y.wait_ge(sem.v, vg)
+    Y.dma_start(out=T.win[15:128:16, 2048:4096], in_=T.win[15:128:16, 0:2048]).then_inc(sem.cp, 16)
+    S.wait_ge(sem.cp, 16)
+    s_gw = act(T.gw[:, :], win.indirect(T.off0[:, :]))
+    V.wait_ge(sem.s, s_at["sf"])
+    ts(T.sumw[:, :], T.g16[:, :], A.is_equal, T.gcol[:, 0:1], A.mult, T.ge8[:, 0:1])
+    ts(T.idf[:, :], T.dl[:, :, :], A.is_equal, 0.0, A.mult, 64.0)
+    v_at["sumf"] = ts(T.sumf[:, :], T.g16[:, :], A.is_equal, T.gcol[:, 0:1], A.mult, T.sf[:, 0:1])
 
-    marks, n = visit(1, s_ex1)
+    vg, v_sc, n = visit(1, v_sc)
     hand_on(1, n)
-    report(1, keep(1, marks, T.vp1))
-    n = add_w(5, part)
-    vw(n)
-    s_ex3 = visitors(3)
+    v_w, n = weights(1, T.mm1, max(vg, v_at["sumf"]), 0)
+    report(1, n)
 
-    marks, n = visit(2, s_ex2)
+    vg, v_sc, n = visit(2, v_sc)
     hand_on(2, n)
-    report(2, keep(2, marks, T.vp2))
+    v_w, n = weights(2, T.mm2, vg, v_w)
+    report(2, n)
+    V.wait_ge(sem.s, s_gw)
+    v_m = tt(T.mw0[:, :], T.gw[:, :], T.mk0[:, :], A.mult)
 
-    marks, n = visit(3, s_ex3)
+    vg, v_sc, n = visit(3, v_sc)
     g.wait_ge(sem.v, n)
     send(T.fin[:, :], T.fo[:, :], 1, "hop4")
 
-    V.wait_ge(sem.s, s_own)
+    v_w, n = weights(0, T.mw0, v_m, v_w)
     V.wait_ge(sem.bg1, landed(-1))
     V.wait_ge(sem.bg2, landed(-2))
-    vw(vcopy(T.hi[:, :], T.hp[:, :]))
-    vw(ts(T.ha[:, :], T.hi[:, :], A.bitwise_and, 511))
-    vw(tt(T.h96[:, :], T.ha[:, 0:96], T.ha[:, 96:192]))
-    vw(tt(T.h48[:, :], T.h96[:, 0:48], T.h96[:, 48:96]))
-    vw(tt(T.h16[:, :], T.h48[:, 0:16], T.h48[:, 16:32]))
-    vw(tt(T.acc[:, :], T.h16[:, :], T.h48[:, 32:48]))
+    n1 = tt(T.acc1[:, :], T.wr1[:, :], T.wr2[:, :])
+    vw(n1)
+    vw(tt(T.acc[:, :], T.acc1[:, :], T.wl0[:, :]))
 
     V.wait_ge(sem.hop4, landed(1))
-    n1 = tt(T.t2[:, :], T.fin[:, 0:16], T.fin[:, 16:32])
-    ts(T.fb[:, :], T.fin[:, 0:16], A.bitwise_and, 7680, A.arith_shift_right, 2)
-    n2 = ts(T.fa[:, :], T.fin[:, 0:16], A.arith_shift_right, 13)
+    ts(T.fa[:, :], T.fin[:, :], A.arith_shift_right, 13)
+    n1 = ts(T.fb[:, :], T.fin[:, :], A.bitwise_and, 7680, A.arith_shift_right, 2)
+    n2 = ts(T.t3[:, :], T.fin[:, :], A.bitwise_and, 511)
     vw(n1)
-    n1 = ts(T.t3[:, :], T.t2[:, :], A.bitwise_and, 511)
+    v_o = tt(T.ol[:, :], T.fa[:, :], T.fb[:, :])
     vw(n2)
-    v_l = tt(T.ol[:, :], T.fa[:, :], T.fb[:, :])
-    vw(n1)
     v_t = tt(T.ot[:, :], T.t3[:, :], T.acc[:, :])
-    Y.wait_ge(sem.v, v_l)
+    Y.wait_ge(sem.v, v_o)
     Y.dma_start(out=T.last[:], in_=T.ol[:, :]).then_inc(sem.outs, 16)
     S.wait_ge(sem.v, v_t)
     S.dma_start(out=T.total[:], in_=T.ot[:, :]).then_inc(sem.outs, 16)
@@ -335,3 +443,5 @@ def rank_program(g, core, T, topo):
     for name in ("loc", "v", "s", "pe", "gi"):
         g.wait_ge(sem[name], cnt[name])
     g.wait_ge(sem.outs, 32)
+    g.wait_ge(sem.lw, 32)
+    g.wait_ge(sem.cp, 16)

@@ -3,34 +3,28 @@ from concourse.mybir import AluOpType as A, ActivationFunctionType as AF
 NV = 4
 BIG = 16777216.0
 FAR = 32768.0
+CUT = 1088
+ZC = 1280
 
-SCRATCH = {"ps%d" % b: ("psum", [128, 32, 16] if b < 4 else [128, 512], "float32") for b in range(8)}
-SCRATCH["srci"] = ("sbuf", [128, 4, 128], "int32")
-SCRATCH["s16"] = ("sbuf", [128, 128, 4], "float16")
-SCRATCH["jj"] = ("sbuf", [128, 128, 4], "float32")
-SCRATCH["lr"] = ("sbuf", [128, 32, 16], "float16")
-SCRATCH["ic"] = ("sbuf", [128, 32, 16], "float32")
-SCRATCH["dl"] = ("sbuf", [128, 8, 16], "float32")
-SCRATCH["kk"] = ("sbuf", [128, 8, 16], "float32")
-for _m in (1, 2, 4):
-    SCRATCH["sh%d" % _m] = ("sbuf", [128, 8, 16], "float16")
+SCRATCH = {"ps%d" % b: ("psum", [128, 512], "float32") for b in range(8)}
+for _n in ("sh1", "sh2", "sh4", "idn", "rep", "repf", "zz", "one", "s1", "sums", "w1", "sumw", "f512", "sumf"):
+    SCRATCH[_n] = ("sbuf", [128, 8, 16], "float16")
+SCRATCH["m16"] = ("sbuf", [128, 2, 8], "float16")
+SCRATCH["lrb"] = ("sbuf", [128, 4, 8, 16], "float16")
 for _dt, _bufs in (
-        ("int32", "pidx 8 pq 8 p3 8 p31 8 p15 8 lst 144 lq 144 ls 144 ei 64 fo 16 fin 16 fa 16 fb 16 t3 16 w0 2048"),
-        ("float16", "y1 144 y2 144 y4 144 sums 128 sumw 128 sumf 128"
-                    " g1 2048 g2 2048 g3 2048 mm0 256 mm1 256 mm2 256 mm3 256 mw0 256"),
-        ("bfloat16", "idb 128 idf 128 far 256 hx0 256 hx1 256 hx2 256"),
+        ("int32", "base 512 lst 128 w0 2048 xi 16 ei 64 fo 16 fin 16 fp 16 ft 16"),
+        ("float16", "b16 512 g1 2048 g2 2048 g3 2048 lf1 128 lf2 128 mm0 256 mm1 256 mm2 256 mm3 256 mw0 256"
+                    " hx0 256 hx1 256 hx2 256 nfar 256 far 256 rr 144 y4 144"),
         ("uint16", "l1 128 l2 128 l4 128 l8 128 eu 64 le1 32 le2 32 le3 16 off0 16 ho0 16 ho1 16 ho2 16"
                    " land1 16 land2 16 land3 16"),
-        ("float32", "f31 8 f15 8 i8 8 f4 8 isl 8 nis 8 sg 8 valc 8 gcol 8 ge8 8 lt8 8 sf 8 c7 8 cn 8 c15 8"
-                    " ay1 144 ay2 144 ay4 144 xk 144 em 16 eh 16 ht 16 mta 16 mtb 16 mt 16 g16 128 l256 256"
-                    " hi0 16 xo 16"
-                    " sd 256 ta 2048 tb 2048 win 4096 mk0 256 mk1 256 mk2 256 mk3 256 sc 256 sw 256 gw 256"
+        ("float32", "mt 16 ht 16 hi0 16 xo 16 sd 256 ta 2048 tb 2048 win 4096"
+                    " mk0 256 mk1 256 mk2 256 mk3 256 sc 256 sw 256 gw 256"
                     " wl0 16 wl1 16 wl2 16 wr1 16 wr2 16 acc1 16 acc 16 ol 16 ot 16")):
     _w = _bufs.split()
     for _i in range(0, len(_w), 2):
         SCRATCH[_w[_i]] = ("sbuf", [128, int(_w[_i + 1])], _dt)
-SEMAPHORES = ["v", "s", "pe", "gi", "lda", "ldb", "lde", "lw", "cp", "outs", "loc",
-              "ad1", "ad2", "ad3", "hop1", "hop2", "hop3", "hop4", "bg1", "bg2"]
+SEMAPHORES = ["v", "s", "pe", "gi", "lda", "ldl", "lde", "lw", "lx1", "lx2", "cp", "outs", "loc",
+              "ad1", "ad2", "ad3", "hop10", "hop11", "hop20", "hop21", "hop30", "hop31", "hop4", "bg1", "bg2"]
 
 
 def rank_program(g, core, T, topo):
@@ -71,116 +65,88 @@ def rank_program(g, core, T, topo):
         ins = PE.matmul(out=out, lhsT=lhsT, rhs=rhs, start=start, stop=stop)
         return done("pe", ins) if count else 0
 
-    Y.dma_start(out=T.lst[:, 0:128], in_=T.nx[:]).then_inc(sem.ldb, 16)
-    S.dma_start(out=T.lst[:, 128:144], in_=T.x[:]).then_inc(sem.ldb, 16)
-    Y.dma_start(out=T.srci[32:64, :, :], in_=T.nx[:]).then_inc(sem.lda, 16)
-    S.dma_start(out=T.srci[64:96, :, :], in_=T.w[:]).then_inc(sem.lda, 16)
-    Y.dma_start(out=T.srci[0:32, :, :], in_=T.nx[:]).then_inc(sem.lda, 16)
-    S.dma_start(out=T.ei[:, :], in_=T.e[:]).then_inc(sem.lde, 16)
-
     def iota(ap, pattern, cm=0, base=0):
         return done("gi", g.iota(ap, pattern, base, cm, allow_small_or_imprecise_dtypes=True))
 
-    g_p = done("gi", g.iota(T.pidx[:, 0:1], [[0, 1]], 0, 1))
-    g_i = iota(T.i8[:, :], [[1, 8]])
-    g_0 = done("gi", g.iota(T.w0[:, 512:1024], [[0, 512]], 0, 0))
-    g_c = iota(T.ic[:, :, :], [[1, 4], [4, 8], [0, 16]])
-    g_x = iota(T.xk[:, :], [[1, 144]], -1)
-    iota(T.dl[:, :, :], [[16, 8], [1, 16]], -1)
-    g_k = iota(T.kk[:, :, :], [[-16, 8], [0, 16]], 1)
-    g_q = done("gi", g.iota(T.pq[:, 0:1], [[0, 1]], 0, 4))
-    g_j = iota(T.jj[:, :, :], [[16, 128], [1, 4]])
-    iota(T.em[:, :], [[0, 2], [1, 8]])
-    iota(T.eh[:, :], [[1, 2], [0, 8]])
-    iota(T.ht[:, :], [[2048, 2], [0, 8]])
-    iota(T.g16[:, :], [[16, 8], [0, 16]])
-    iota(T.l256[:, :], [[0, 16], [1, 16]])
-    g_l = iota(T.sd[:, :], [[0, 256]])
+    def sel(out, in_, pattern, op, c, base, cm):
+        return done("gi", g.affine_select(out, in_, pattern, op, c, base, cm))
 
-    n = fill(T.w0[:, 0:512], 0)
-    S.wait_ge(sem.v, n)
-    for q in (2, 3):
-        s_0 = act(T.w0[:, 512 * q:512 * q + 512], T.w0[:, 0:512])
-    Y.wait_ge(sem.v, n)
-    Y.wait_ge(sem.s, s_0)
-    Y.wait_ge(sem.gi, g_0)
+    ps = [T["ps%d" % b] for b in range(8)]
+    cols = lambda t, q: t[:, 512 * q:512 * q + 512]
+    al = lambda name: T[name][:, :, :]
+
+    Y.dma_start(out=T.lst[:, :], in_=T.nx[:]).then_inc(sem.ldl, 16)
+    S.dma_start(out=T.base[32:64, :], in_=T.w[:]).then_inc(sem.lda, 16)
+    Y.dma_start(out=T.base[0:32, :], in_=T.nx[:]).then_inc(sem.lda, 16)
+    S.dma_start(out=T.ei[:, :], in_=T.e[:]).then_inc(sem.lde, 16)
+    Y.dma_start(out=T.xi[:, :], in_=T.x[:]).then_inc(sem.lde, 16)
+
+    v_z = fill(T.w0[:, 0:256], 0)
+    v_lr = fill(T.lrb[0:68, :, :, :], 0.0)
+    v_w0 = fill(T.w0[:, 256:ZC], 0)
+    S.wait_ge(sem.v, v_z)
+    for c in range(ZC, 2048, 256):
+        s_w0 = act(T.w0[:, c:c + 256], T.w0[:, 0:256])
+    Y.wait_ge(sem.v, v_w0)
+    Y.wait_ge(sem.s, s_w0)
+    Y.dma_start(out=T.w0[1:128:16, :], in_=T.nx[:]).then_inc(sem.lw, 16)
     Y.dma_start(out=T.w0[8:128:16, :], in_=T.w[:]).then_inc(sem.lw, 16)
-    S.wait_ge(sem.ldb, 32)
-    for i in range(0, 32, 8):
-        s_lr = act(T.lr[:, i:i + 8, :], T.lst[:, 0:128], AF.Copy, 0.0, 0.0)
-    fill(T.valc[0:32, 0:1], 16.0)
-    fill(T.valc[32:64, 0:1], -2047.0 / 128)
-    V.wait_ge(sem.gi, g_p)
-    n1 = ts(T.p31[:, 0:1], T.pidx[:, 0:1], A.bitwise_and, 31)
-    n2 = ts(T.p15[:, 0:1], T.pidx[:, 0:1], A.bitwise_and, 15)
-    vw(n1)
-    vcopy(T.f31[:, 0:1], T.p31[:, 0:1])
-    vw(n2)
-    n2 = vcopy(T.f15[:, 0:1], T.p15[:, 0:1])
+    g_b = iota(T.base[64:68, :], [[1, 512]], 512)
 
-    V.wait_ge(sem.ldb, 32)
-    n = ts(T.lq[:, :], T.lst[:, :], A.mult, 2049)
-    v_l = vcopy(T.l1[:, :], T.lst[:, 0:128])
+    V.wait_ge(sem.ldl, 16)
+    v_l = vcopy(T.l1[:, :], T.lst[:, :])
+    V.wait_ge(sem.lda, 32)
+    V.wait_ge(sem.gi, g_b)
+    v_b = vcopy(T.b16[0:68, 0:256], T.base[0:68, 0:256])
+    S.wait_ge(sem.lda, 32)
+    S.wait_ge(sem.gi, g_b)
+    s_b = act(T.b16[0:68, 256:512], T.base[0:68, 256:512])
+
+    fill(al("sh1"), 0.0)
+    n = fill(T.rr[:, :], 0.0)
     vw(n)
-    v_c = ts(T.ls[:, :], T.lq[:, :], A.arith_shift_right, 7, A.bitwise_and, 2047)
-    Y.wait_ge(sem.v, v_c)
-    Y.dma_start(out=T.w0[1:128:16, :], in_=T.ls[:, 0:128]).then_inc(sem.lw, 16)
+    v_rr = fill(T.rr[:, 15:144:16], 1.0)
+    v_s2 = fill(al("sh2"), 0.0)
+    V.wait_ge(sem.lde, 32)
+    v_eu = vcopy(T.eu[:, :], T.ei[:, :])
+    S.wait_ge(sem.v, v_rr)
+    for name in ("sh4", "zz"):
+        act(al(name), T.rr[:, 0:128], AF.Copy, 0.0, 0.0)
+    s_c = act(al("one"), T.rr[:, 0:128], AF.Copy, 1.0, 0.0)
 
-    V.wait_ge(sem.lda, 48)
-    for c0 in (0, 64):
-        n = ts(T.srci[32:64, :, c0:c0 + 64], T.srci[32:64, :, c0:c0 + 64], A.bitwise_and, 1920)
-        S.wait_ge(sem.v, n)
-        for i2 in (2, 3):
-            s_16 = act(T.s16[0:96, c0:c0 + 64, i2], T.srci[0:96, i2, c0:c0 + 64])
-    v_and = n
-    V.wait_ge(sem.gi, g_i)
-    v_is = ts(T.isl[:, :], T.i8[:, :], A.is_equal, T.f15[:, 0:1])
-    V.wait_ge(sem.gi, g_c)
-    V.wait_ge(sem.s, s_lr)
-    ts(T.lr[64:96, :, 8:16], T.ic[64:96, :, 8:16], A.is_equal, T.f31[64:96, 0:1])
-    ts(T.lr[96:128, :, 0:1], T.ic[96:128, :, 0:1], A.is_equal, T.f31[96:128, 0:1])
-    ts(T.lr[0:64, :, 1:2], T.ic[0:64, :, 1:2], A.is_equal, T.f31[0:64, 0:1], A.mult, T.valc[0:64, 0:1])
-    vw(v_and)
-    for i2 in (0, 1):
-        v_16 = vcopy(T.s16[0:96, :, i2], T.srci[0:96, i2, :])
-
-    s_sh = {}
-    s_y = {}
-
-    def zero(m):
-        s_sh[m] = act(T["sh%d" % m][:, :, :], T.lst[:, 0:128], AF.Copy, 0.0, 0.0)
-
-    def diag(m):
-        n = act(T["ay%d" % m][:, :], T.xk[:, :], AF.Abs, m - 15.0)
-        S.wait_ge(sem.s, n)
-        s_y[m] = act(T["y%d" % m][:, :], T["ay%d" % m][:, :], AF.Relu, T.isl[:, m:m + 1], T.nis[:, m:m + 1])
-
-    zero(1)
-    zero(2)
-    S.wait_ge(sem.v, v_is)
-    nis = act(T.nis[:, :], T.isl[:, :], AF.Copy, 0.0, -1.0)
+    g.wait_ge(sem.v, v_lr)
+    for rows, r0, r1, pattern in (((0, 32), 1, 2, [[-1, 4], [-4, 8], [0, 1]]),
+                                  ((64, 68), 0, 1, [[-1, 4], [0, 8], [0, 1]]),
+                                  ((32, 64), 8, 16, [[-1, 4], [-4, 8], [0, 8]])):
+        g.wait_ge(sem.gi, cnt["gi"])
+        ap = T.lrb[rows[0]:rows[1], :, :, r0:r1]
+        g_lr = sel(ap, ap, pattern, A.not_equal, 1.0, 0, 1)
+    g.wait_ge(sem.gi, g_lr)
 
     def shifts(m):
         sh = T["sh%d" % m]
-        V.wait_ge(sem.s, s_sh[m])
-        n = ts(sh[:, :, m + 1:min(2 * m + 1, 8)], T.dl[:, :, m + 1:min(2 * m + 1, 8)], A.is_equal, float(m))
         k = 8 + 2 * m if m > 1 else 9
-        if m > 1:
-            n = ts(sh[:, :, 8 + m:k], T.dl[:, :, 8 + m:k], A.is_equal, float(m))
-        if m < 4:
-            n = ts(sh[:, :, k:16], T.kk[:, :, k:16], A.is_equal, 7.0 + m)
+        for r0, r1 in ((m + 1, min(2 * m + 1, 8)), (8 + m, k)):
+            if r1 > r0:
+                n = sel(sh[:, :, r0:r1], sh[:, :, r0:r1], [[-16, 8], [-1, r1 - r0]], A.not_equal, 1.0, m - r0, 1)
+        if k < 16:
+            n = sel(sh[:, :, k:16], sh[:, :, k:16], [[-16, 8], [0, 16 - k]], A.not_equal, 1.0, -7 - m, 1)
         return n
 
-    v_sh = {}
-
-    ps = [T["ps%d" % b] for b in range(8)]
-    full = lambda q: ps[q][:, :, :]
-    cols = lambda t, q: t[:, 512 * q:512 * q + 512]
-
-    def first(q, k0, k1):
-        for h in range(4):
-            mm(ps[q][:, :, 4 * h:4 * h + 4], T.lr[k0:k1, 8 * h:8 * h + 8, :], T.s16[k0:k1, 32 * q:32 * q + 32, :],
-               h == 0, False, False)
+    g.wait_ge(sem.v, v_rr)
+    g_sh = {1: shifts(1)}
+    g.wait_ge(sem.v, v_s2)
+    g_sh[2] = shifts(2)
+    g.wait_ge(sem.s, s_c)
+    g_ht = iota(T.ht[:, :], [[2048, 2], [0, 8]])
+    sel(T.rep[0:16, :, :], T.zz[0:16, :, :], [[0, 8], [1, 16]], A.not_equal, 1.0, 0, -1)
+    n = sel(T.m16[0:16, :, :], T.zz[0:16, 0:2, 0:8], [[0, 2], [1, 8]], A.not_equal, 1.0, 0, -1)
+    g.wait_ge(sem.gi, n)
+    n = sel(T.m16[0:16, :, 1:8], T.m16[0:16, :, 1:8], [[0, 2], [1, 7]], A.not_equal, 1.0, 8, -1)
+    g.wait_ge(sem.gi, n)
+    g_m = sel(T.m16[0:16, 1:2, :], T.m16[0:16, 1:2, :], [[0, 1], [0, 8]], A.not_equal, 1.0, 15, -1)
+    g_sh[4] = shifts(4)
+    g_y = sel(T.y4[:, :], T.rr[:, :], [[-16, 9], [0, 16]], A.is_equal, 0.0, -4, 1)
 
     def send(out, src, d, name):
         dst = peer(d)
@@ -191,198 +157,190 @@ def rank_program(g, core, T, topo):
     def landed(d):
         return len(topo.engines(peer(-d), core))
 
-    v_at = {}
-    s_at = {}
-
-    def vector_extra(m):
-        if m == 1:
-            V.wait_ge(sem.gi, g_q)
-            n = ts(T.p3[:, 0:1], T.pq[:, 0:1], A.bitwise_and, 12)
-            V.wait_ge(sem.lde, 16)
-            v_at["eu"] = vcopy(T.eu[:, :], T.ei[:, :])
-            vw(n)
-            v_at["f4"] = vcopy(T.f4[:, 0:1], T.p3[:, 0:1])
-            v_sh[2] = shifts(2)
-        elif m == 2:
-            n = ts(T.hi0[:, :], T.ei[:, 0:16], A.is_ge, 8, A.mult, 2048.0)
-            tt(T.gcol[:, 0:1], T.pidx[:, 0:1], T.p15[:, 0:1], A.subtract)
-            v_sh[4] = shifts(4)
-            vw(n)
-            n = tt(T.xo[:, :], T.ls[:, 128:144], T.hi0[:, :])
-            ts(T.idb[:, :], T.dl[:, :, :], A.is_equal, 0.0)
-            vw(n)
-            vcopy(T.off0[:, :], T.xo[:, :])
-        else:
-            V.wait_ge(sem.gi, g_l)
-            V.wait_ge(sem.s, s_at["lt8"])
-            ts(T.mta[:, :], T.em[:, :], A.is_equal, T.cn[:, 0:1])
-            n = ts(T.mtb[:, :], T.eh[:, :], A.mult, T.c15[:, 0:1])
-            fill(T.sd[:, 0:256:16], -BIG)
-            vw(n)
-            v_at["mt"] = tt(T.mt[:, :], T.mta[:, :], T.mtb[:, :])
-            ts(T.sums[:, :], T.g16[:, :], A.is_equal, T.gcol[:, 0:1], A.mult, T.lt8[:, 0:1])
-            v_at["far"] = ts(T.far[:, :], T.l256[:, :], A.not_equal, T.f15[:, 0:1], A.mult, -FAR)
-
-    def scalar_extra(m):
-        if m == 1:
-            diag(2)
-            zero(4)
-            S.wait_ge(sem.gi, g_j)
-            S.wait_ge(sem.v, v_at["f4"])
-            s_at["id"] = act(T.s16[96:128, :, :], T.jj[96:128, :, :], AF.Identity, T.f4[96:128, 0:1])
-        elif m == 2:
-            diag(4)
-            n = act(T.sg[:, 0:1], T.f15[:, 0:1], AF.Sign, -7.5)
-            act(T.c15[:, 0:1], T.f15[:, 0:1], AF.Relu, -14.0)
-            S.wait_ge(sem.s, n)
-            n = act(T.c7[:, 0:1], T.sg[:, 0:1], AF.Copy, -3.5, -3.5)
-            S.wait_ge(sem.s, n)
-            act(T.cn[:, 0:1], T.f15[:, 0:1], AF.Identity, T.c7[:, 0:1])
-            s_at["lt8"] = act(T.lt8[:, 0:1], T.sg[:, 0:1], AF.Copy, 0.5, -0.5)
-        else:
-            S.wait_ge(sem.v, v_at["mt"])
-            act(T.mk0[:, :], T.mt[:, :].indirect(T.eu[:, 0:16]))
+    g.wait_ge(sem.v, v_eu)
+    for t in (1, 2, 3):
+        send(T["le%d" % t][:, :], T.eu[:, 16 * t:min(16 * t + 32, 64)], t, "ad%d" % t)
 
     tabs = {1: (T.w0, T.tb), 2: (T.tb, T.ta), 4: (T.ta, T.win)}
-    lists = {1: T.l1, 2: T.l2, 4: T.l4, 8: T.l8}
+    lists = {1: T.l1, 2: T.l2, 4: T.l4}
     gs = {1: T.g1, 2: T.g2, 4: T.g3}
-    v_l = {1: v_l, 0: v_l}
-    v_ev, s_ev = v_l[0], s_0
+    banks = {1: (0, 1, 2, 3), 2: (0, 1, 5, 7), 4: (0, 1, 2, 3)}
+    mine = {1: (0, 1), 2: (0, 1), 4: (0, 2, 1)}
+    v_ev, s_ev = v_w0, s_w0
     for m in (1, 2, 4):
         old, new = tabs[m]
-        G, L, Ln, sh = gs[m], lists[m], lists[2 * m], T["sh%d" % m]
+        G, L, sh, bank = gs[m], lists[m], al("sh%d" % m), [ps[b] for b in banks[m]]
         ind = lambda q: old[:, 0:2048].indirect(L[:, 32 * q:32 * q + 32])
         if m == 1:
             V.wait_ge(sem.lw, 32)
             S.wait_ge(sem.lw, 32)
-        vw(max(v_ev, v_l[0]))
+        vw(max(v_ev, v_l))
         V.wait_ge(sem.s, s_ev)
-        vg = {0: vcopy(cols(G, 0), ind(0))}
-        if m == 1:
-            V.wait_ge(sem.gi, g_k)
-            v_sh[1] = shifts(1)
-        vg[1] = vcopy(cols(G, 1), ind(1))
-        S.wait_ge(sem.v, max(v_ev, v_l[1]))
+        S.wait_ge(sem.v, max(v_ev, v_l))
         S.wait_ge(sem.s, s_ev)
-        sg = {q: act(cols(G, q), ind(q)) for q in (2, 3)}
-        if m == 1:
-            S.wait_ge(sem.gi, g_x)
-            S.wait_ge(sem.s, nis)
-            diag(1)
+        got = {}
+        for q in (0, 2):
+            got[q] = vcopy(cols(G, q), ind(q))
+        for q in (1, 3):
+            got[q] = act(cols(G, q), ind(q))
+        if m < 4:
+            Y.wait_ge(sem.v, got[2])
+            Y.wait_ge(sem.s, got[3])
+            Y.dma_start(out=T["lf%d" % m][:, :], in_=G[m:128:16, :]).then_inc(sem["lx%d" % m], 16)
 
         if m == 1:
-            PE.wait_ge(sem.v, v_16)
-            PE.wait_ge(sem.s, s_16)
-            for q in range(4):
-                first(q, 0, 96)
-            PE.wait_ge(sem.v, v_sh[1])
-        else:
-            PE.wait_ge(sem.v, max(v_ev, v_sh[m]))
-            PE.wait_ge(sem.s, s_ev)
-            for q in (2, 3):
-                first(q, 0, 96 if m == 2 else 128)
-                mm(full(q), T.sh1[:, :, :], cols(T.g1, q), False, False, False)
-                if m > 2:
-                    mm(full(q), T.sh2[:, :, :], cols(T.g2, q), False, False, False)
-            if m == 2:
-                PE.wait_ge(sem.s, s_at["id"])
-                for q in (0, 1):
-                    first(q, 96, 128)
+            PE.wait_ge(sem.v, v_b)
+            PE.wait_ge(sem.s, s_b)
+            PE.wait_ge(sem.gi, g_lr)
+        for q in (0, 2, 1, 3):
+            if m == 1 or q not in mine[m]:
+                mm(bank[q][:, :], T.lrb[0:68, q, :, :], T.b16[0:68, :], True, False, False)
 
-        def extract(half):
+        def moves(m, q, f, lhsT, out, start, stop):
+            G = gs[m]
             n = 0
-            for b in range(16):
-                n = mm(ps[4 + half][:, 0:64], T["y%d" % m][:, 15 - b:143 - b],
-                       G[:, 1024 * half + b:1024 * half + 1024:16], b == 0, b == 15, b == 15)
+            if m == 1:
+                todo = [(out[:, 128 * (i % 4) + 64 * f:128 * (i % 4) + 64 * f + 64], G[:, 1024 * f + i:1024 * f + 1024:16])
+                        for i in range(4 * q, 4 * q + 4)]
+            elif m == 2:
+                todo = [(out[:, x:512:8], G[:, 256 * x + 64 * q:256 * x + 64 * q + 64]) for x in range(4 * f, 4 * f + 4)]
+            else:
+                todo = [(out[:, :], G[:, 1024 * f + q // 2:1024 * f + 1024:2])] if q % 2 == f else []
+            for i, (o, r) in enumerate(todo):
+                last = stop and i == len(todo) - 1
+                n = mm(o, lhsT, r, start and i == 0, last, last)
             return n
 
+        for q in range(4):
+            if m > 1 and q not in mine[m]:
+                for k in (1, 2):
+                    if k < m:
+                        for f in (0, 1):
+                            moves(k, q, f, al("sh%d" % k), bank[q], False, False)
+        PE.wait_ge(sem.gi, g_sh[m])
         pc = {}
-        for q in (0, 2, 1, 3):
-            if q < 2:
-                PE.wait_ge(sem.v, vg[q])
-            else:
-                PE.wait_ge(sem.s, sg[q])
-            pc[q] = mm(full(q), sh[:, :, :], cols(G, q), q < 2 and m == 4, True)
-        PE.wait_ge(sem.s, s_y[m])
-        px = {h: extract(h) for h in (1, 0)}
-        for q in (2, 3):
-            S.wait_ge(sem.pe, pc[q])
-            s_ev = act(cols(new, q), full(q))
-        for q in (0, 1):
+        for f in (0, 1):
+            PE.wait_ge(sem.v, got[2 * f])
+            PE.wait_ge(sem.s, got[2 * f + 1])
+            for q in (0, 2, 1, 3):
+                fresh = m > 1 and q in mine[m]
+                n = moves(m, q, f, sh, bank[q], fresh and (f == 0 or m == 4), f == 1 or m == 4)
+                if n:
+                    pc[q] = n
+        if m == 4:
+            s_nf = act(T.nfar[0:16, :], T.b16[0:16, 0:256], AF.Copy, -FAR, 0.0)
+            S.wait_ge(sem.gi, g_ht)
+            S.wait_ge(sem.v, v_eu)
+            s_hx = {0: act(T.hx0[:, :], T.ht[:, :].indirect(T.eu[:, 16:32])), 3: 0}
+        for q in mine[m]:
             V.wait_ge(sem.pe, pc[q])
-            v_ev = tt(cols(new, q), cols(old, q), full(q)) if m > 1 else vcopy(cols(new, q), full(q))
-        vector_extra(m)
-        scalar_extra(m)
-        for h in (1, 0):
-            V.wait_ge(sem.pe, px[h])
-            v_l[h] = vcopy(Ln[:, 64 * h:64 * h + 64], ps[4 + h][:, 0:64])
+            v_ev = tt(cols(new, q), cols(old, q), bank[q][:, :]) if m > 1 else vcopy(cols(new, q), bank[q][:, :])
+        for q in range(4):
+            if q not in mine[m]:
+                S.wait_ge(sem.pe, pc[q])
+                s_ev = act(cols(new, q), bank[q][:, :])
+        if m < 4:
+            V.wait_ge(sem["lx%d" % m], 16)
+            v_l = vcopy(lists[2 * m][:, :], T["lf%d" % m][:, :])
         if m == 1:
-            g.wait_ge(sem.v, v_at["eu"])
-            for t in (1, 2, 3):
-                send(T["le%d" % t][:, :], T.eu[:, 16 * t:min(16 * t + 32, 64)], t, "ad%d" % t)
+            PE.wait_ge(sem.gi, g_m)
+            p_mt = mm(ps[6][:, 0:16], T.rep[0:16, :, :], T.m16[0:16, :, :], True, True)
+
+    PE.wait_ge(sem.gi, g_y)
+    for h in (0, 1):
+        for b in range(16):
+            px = mm(ps[4][:, 64 * h:64 * h + 64], T.y4[:, 15 - b:143 - b], T.g3[:, 2 * b + h:2048:32], b == 0, b == 15, b == 15)
+
+    V.wait_ge(sem.pe, p_mt)
+    v_mt = vcopy(T.mt[:, :], ps[6][:, 0:16])
+    n = ts(T.hi0[:, :], T.ei[:, 0:16], A.is_ge, 8, A.mult, 2048.0)
+    vw(n)
+    n = tt(T.xo[:, :], T.xi[:, :], T.hi0[:, :])
+    vw(n)
+    vcopy(T.off0[:, :], T.xo[:, :])
+    S.wait_ge(sem.v, v_mt)
+    act(T.mk0[:, 0:128], T.mt[:, :].indirect(T.eu[:, 0:8]))
+    V.wait_ge(sem.pe, px)
+    v_l = vcopy(T.l8[:, :], ps[4][:, 0:128])
+
+    n = sel(al("s1"), al("one"), [[16, 8], [0, 16]], A.is_ge, 0.0, 7, -1)
+    n2 = iota(T.sd[:, :], [[0, 256]])
+    sel(al("idn"), al("zz"), [[-16, 8], [-1, 16]], A.not_equal, 1.0, 0, 1)
+    g.wait_ge(sem.gi, n)
+    sel(al("sums"), al("s1"), [[-16, 8], [0, 16]], A.is_ge, 0.0, 0, 1)
+    g.wait_ge(sem.gi, n2)
+    sel(T.sd[:, :], T.sd[:, :], [[0, 16], [1, 16]], A.not_equal, -BIG, 0, 0)
+    n = sel(al("w1"), al("one"), [[16, 8], [0, 16]], A.is_ge, 0.0, 15, -1)
+    g.wait_ge(sem.s, s_nf)
+    g_v = sel(T.far[0:16, :], T.nfar[0:16, :], [[0, 16], [1, 16]], A.not_equal, 0.0, 0, -1)
+    g.wait_ge(sem.gi, n)
+    sel(al("sumw"), al("w1"), [[-16, 8], [0, 16]], A.is_ge, 0.0, -8, 1)
+    g_w = sel(T.repf[0:16, :, :], T.zz[0:16, :, :], [[0, 8], [1, 16]], A.not_equal, 64.0, 0, -1)
 
     win = T.win[:, 0:4096]
-    ind = lambda q: T.win[:, 0:2048].indirect(T.l8[:, 32 * q:32 * q + 32])
-    vw(v_l[0])
+    vw(max(v_ev, v_l))
     V.wait_ge(sem.s, s_ev)
-    for q in (0, 1):
-        n = vcopy(cols(T.win, 4 + q), ind(q))
-    S.wait_ge(sem.v, v_l[1])
+    S.wait_ge(sem.v, v_l)
     S.wait_ge(sem.s, s_ev)
-    for q in (2, 3):
-        s_w = act(cols(T.win, 4 + q), ind(q))
+    n = vcopy(T.win[:, 2048:2048 + CUT], T.win[:, 0:2048].indirect(T.l8[:, 0:CUT // 16]))
+    s_w = act(T.win[:, 2048 + CUT:4096], T.win[:, 0:2048].indirect(T.l8[:, CUT // 16:128]))
     vw(n)
     V.wait_ge(sem.s, s_w)
 
-    s_at[0] = act(T.hx0[:, :], T.ht[:, :].indirect(T.eu[:, 16:32]))
-    act(T.ge8[:, 0:1], T.sg[:, 0:1], AF.Copy, 0.5, 0.5)
-    s_at["sf"] = act(T.sf[:, 0:1], T.sg[:, 0:1], AF.Copy, 256.5, -255.5)
+    s_mk = {0: act(T.mk0[:, 128:256], T.mt[:, :].indirect(T.eu[:, 8:16]))}
     for t in (1, 2, 3):
         S.wait_ge(sem["ad%d" % t], landed(t))
         le = T["le%d" % t]
-        s_at[t] = act(T["mk%d" % t][:, :], T.mt[:, :].indirect(le[:, 0:16]))
+        s_mk[t] = act(T["mk%d" % t][:, :], T.mt[:, :].indirect(le[:, 0:16]))
         if t < 3:
-            s_at[t] = act(T["hx%d" % t][:, :], T.ht[:, :].indirect(le[:, 16:32]))
+            s_hx[t] = act(T["hx%d" % t][:, :], T.ht[:, :].indirect(le[:, 16:32]))
+
+    half = lambda t, h: t[:, 128 * h:128 * h + 128]
+    part = lambda t, h: t[:, 8 * h:8 * h + 8]
 
     def visit(t, v_free):
         off = T["land%d" % t] if t else T.off0
-        M, mk = T["mm%d" % t], T["mk%d" % t]
+        M, mk, fin = T["mm%d" % t], T["mk%d" % t], t == 3
         if t:
-            V.wait_ge(sem.s, s_at[t])
+            V.wait_ge(sem.s, s_mk[t])
         if t == 1:
             V.wait_ge(sem.cp, 16)
-        if t:
-            V.wait_ge(sem["hop%d" % t], landed(1))
-        vg = [tt(M[:, 128 * h:128 * h + 128], win.indirect(off[:, 8 * h:8 * h + 8]), mk[:, 128 * h:128 * h + 128], A.mult)
-              for h in (0, 1)]
-        PE.wait_ge(sem.v, max(v_free, v_at["far"]) if t < 3 else max(v_free, v_at["sumf"]))
-        if t < 3:
-            PE.wait_ge(sem.s, s_at[t])
+        vg = []
         for h in (0, 1):
-            mm(ps[6 + h][:, 0:128], (T.idb if t < 3 else T.idf)[:, :], T.far[:, 0:128], True, False, False)
-            if t < 3:
-                mm(ps[6 + h][:, 0:128], T.idb[:, :], T["hx%d" % t][:, 128 * h:128 * h + 128], False, False, False)
+            if t:
+                V.wait_ge(sem["hop%d%d" % (t, h)], landed(1))
+            elif h:
+                V.wait_ge(sem.s, s_mk[0])
+            vg.append(tt(half(M, h), win.indirect(part(off, h)), half(mk, h), A.mult))
+        PE.wait_ge(sem.v, v_free)
+        PE.wait_ge(sem.gi, g_v if t == 0 else g_w)
+        PE.wait_ge(sem.s, s_hx[t])
+        for h in (0, 1):
+            mm(ps[6 + h][:, 0:128], (T.repf if fin else T.rep)[0:16, :, :], T.far[0:16, 0:128], True, False, False)
+            if not fin:
+                mm(ps[6 + h][:, 0:128], al("idn"), half(T["hx%d" % t], h), False, False, False)
         pr = []
         for h in (0, 1):
             PE.wait_ge(sem.v, vg[h])
-            pr.append(mm(ps[6 + h][:, 0:128], (T.sums if t < 3 else T.sumf)[:, :], M[:, 128 * h:128 * h + 128],
-                         False, True))
+            pr.append(mm(ps[6 + h][:, 0:128], al("sumf" if fin else "sums"), half(M, h), False, True))
+        out = T.fo if fin else T["ho%d" % t]
+        if t == 0:
+            V.wait_ge(sem.gi, g_v)
         for h in (0, 1):
             V.wait_ge(sem.pe, pr[h])
-            n = done("v", V.tensor_tensor_scan(out=T.sc[:, 128 * h:128 * h + 128], data0=T.sd[:, 0:128],
+            n = done("v", V.tensor_tensor_scan(out=half(T.sc, h), data0=T.sd[:, 0:128],
                                                data1=ps[6 + h][:, 0:128], initial=0.0, op0=A.add, op1=A.max))
-        vw(n)
-        out = T["ho%d" % t] if t < 3 else T.fo
-        return vg[1], n, vcopy(out[:, :], T.sc[:, 15:256:16])
-
-    def hand_on(t, n):
-        g.wait_ge(sem.v, n)
-        send(T["land%d" % (t + 1)][:, :], T["ho%d" % t][:, :], 1, "hop%d" % (t + 1))
+            vw(n)
+            c = vcopy(part(out, h), T.sc[:, 128 * h + 15:128 * h + 128:16])
+            if not fin:
+                g.wait_ge(sem.v, c)
+                send(part(T["land%d" % (t + 1)], h), part(out, h), 1, "hop%d%d" % (t + 1, h))
+        return vg[1], c
 
     def weights(t, M, n, v_free):
         PE.wait_ge(sem.v, max(n, v_free))
-        mm(ps[4][:, 0:256], T.idb[:, :], T.far[:, :], True, False, False)
-        p = mm(ps[4][:, 0:256], T.sumw[:, :], M[:, :], False, True)
+        mm(ps[4][:, 0:256], T.rep[0:16, :, :], T.far[0:16, :], True, False, False)
+        p = mm(ps[4][:, 0:256], al("sumw"), M[:, :], False, True)
         V.wait_ge(sem.pe, p)
         n = done("v", V.tensor_tensor_scan(out=T.sw[:, :], data0=T.sd[:, :], data1=ps[4][:, 0:256],
                                            initial=0.0, op0=A.add, op1=A.max))
@@ -393,31 +351,28 @@ def rank_program(g, core, T, topo):
         g.wait_ge(sem.v, n)
         send(T["wr%d" % t][:, :], T["wl%d" % t][:, :], -t, "bg%d" % t)
 
-    vg, v_sc, n = visit(0, max(v_l.values()))
-    hand_on(0, n)
+    vg, c = visit(0, v_l)
     Y.wait_ge(sem.v, vg)
     Y.dma_start(out=T.win[15:128:16, 2048:4096], in_=T.win[15:128:16, 0:2048]).then_inc(sem.cp, 16)
     S.wait_ge(sem.cp, 16)
     s_gw = act(T.gw[:, :], win.indirect(T.off0[:, :]))
-    V.wait_ge(sem.s, s_at["sf"])
-    ts(T.sumw[:, :], T.g16[:, :], A.is_equal, T.gcol[:, 0:1], A.mult, T.ge8[:, 0:1])
-    ts(T.idf[:, :], T.dl[:, :, :], A.is_equal, 0.0, A.mult, 64.0)
-    v_at["sumf"] = ts(T.sumf[:, :], T.g16[:, :], A.is_equal, T.gcol[:, 0:1], A.mult, T.sf[:, 0:1])
+    V.wait_ge(sem.gi, g_w)
+    n = ts(al("f512"), al("sums"), A.mult, 512.0)
+    vw(n)
+    v_sf = tt(al("sumf"), al("f512"), al("sumw"))
 
-    vg, v_sc, n = visit(1, v_sc)
-    hand_on(1, n)
-    v_w, n = weights(1, T.mm1, max(vg, v_at["sumf"]), 0)
+    vg, c = visit(1, c)
+    v_w, n = weights(1, T.mm1, vg, 0)
     report(1, n)
 
-    vg, v_sc, n = visit(2, v_sc)
-    hand_on(2, n)
+    vg, c = visit(2, c)
     v_w, n = weights(2, T.mm2, vg, v_w)
     report(2, n)
     V.wait_ge(sem.s, s_gw)
     v_m = tt(T.mw0[:, :], T.gw[:, :], T.mk0[:, :], A.mult)
 
-    vg, v_sc, n = visit(3, v_sc)
-    g.wait_ge(sem.v, n)
+    vg, c = visit(3, max(c, v_sf))
+    g.wait_ge(sem.v, c)
     send(T.fin[:, :], T.fo[:, :], 1, "hop4")
 
     v_w, n = weights(0, T.mw0, v_m, v_w)
@@ -428,20 +383,18 @@ def rank_program(g, core, T, topo):
     vw(tt(T.acc[:, :], T.acc1[:, :], T.wl0[:, :]))
 
     V.wait_ge(sem.hop4, landed(1))
-    ts(T.fa[:, :], T.fin[:, :], A.arith_shift_right, 13)
-    n1 = ts(T.fb[:, :], T.fin[:, :], A.bitwise_and, 7680, A.arith_shift_right, 2)
-    n2 = ts(T.t3[:, :], T.fin[:, :], A.bitwise_and, 511)
+    n1 = ts(T.ft[:, :], T.fin[:, :], A.bitwise_and, 511)
+    n2 = ts(T.fp[:, :], T.fin[:, :], A.arith_shift_right, 9)
     vw(n1)
-    v_o = tt(T.ol[:, :], T.fa[:, :], T.fb[:, :])
-    vw(n2)
-    v_t = tt(T.ot[:, :], T.t3[:, :], T.acc[:, :])
-    Y.wait_ge(sem.v, v_o)
-    Y.dma_start(out=T.last[:], in_=T.ol[:, :]).then_inc(sem.outs, 16)
-    S.wait_ge(sem.v, v_t)
-    S.dma_start(out=T.total[:], in_=T.ot[:, :]).then_inc(sem.outs, 16)
+    v_t = tt(T.ot[:, :], T.ft[:, :], T.acc[:, :])
+    S.wait_ge(sem.v, n2)
+    n = act(T.ol[:, :], T.fp[:, :])
+    S.wait_ge(sem.s, n)
+    S.dma_start(out=T.last[:], in_=T.ol[:, :]).then_inc(sem.outs, 16)
+    Y.wait_ge(sem.v, v_t)
+    Y.dma_start(out=T.total[:], in_=T.ot[:, :]).then_inc(sem.outs, 16)
 
     for name in ("loc", "v", "s", "pe", "gi"):
         g.wait_ge(sem[name], cnt[name])
-    g.wait_ge(sem.outs, 32)
-    g.wait_ge(sem.lw, 32)
-    g.wait_ge(sem.cp, 16)
+    for name, n in (("outs", 32), ("lw", 32), ("cp", 16), ("lx1", 16), ("lx2", 16), ("lda", 32), ("ldl", 16), ("lde", 32)):
+        g.wait_ge(sem[name], n)

from concourse.mybir import AluOpType as A, ActivationFunctionType as AF

NV = 4
BIG = 16777216.0
FAR = 32768.0
CUT = 1088
ZC = 1280

SCRATCH = {"ps%d" % b: ("psum", [128, 512], "float32") for b in range(8)}
for _n in ("sh1", "sh2", "sh4", "idn", "rep", "repf", "zz", "one", "s1", "sums", "w1", "sumw", "f512", "sumf"):
    SCRATCH[_n] = ("sbuf", [128, 8, 16], "float16")
SCRATCH["m16"] = ("sbuf", [128, 2, 8], "float16")
SCRATCH["lrb"] = ("sbuf", [128, 4, 8, 16], "float16")
for _dt, _bufs in (
        ("int32", "base 512 lst 128 w0 2048 xi 16 ei 64 fo 16 fin 16 fp 16 ft 16"),
        ("float16", "b16 512 g1 2048 g2 2048 g3 2048 lf1 128 lf2 128 mm0 256 mm1 256 mm2 256 mm3 256 mw0 256"
                    " hx0 256 hx1 256 hx2 256 nfar 256 far 256 rr 144 y4 144"),
        ("uint16", "l1 128 l2 128 l4 128 l8 128 eu 64 le1 32 le2 32 le3 16 off0 16 ho0 16 ho1 16 ho2 16"
                   " land1 16 land2 16 land3 16"),
        ("float32", "mt 16 ht 16 hi0 16 xo 16 sd 256 ta 2048 tb 2048 win 4096"
                    " mk0 256 mk1 256 mk2 256 mk3 256 sc 256 sw 256 gw 256"
                    " wl0 16 wl1 16 wl2 16 wr1 16 wr2 16 acc1 16 acc 16 ol 16 ot 16")):
    _w = _bufs.split()
    for _i in range(0, len(_w), 2):
        SCRATCH[_w[_i]] = ("sbuf", [128, int(_w[_i + 1])], _dt)
SEMAPHORES = ["v", "s", "pe", "gi", "lda", "ldl", "lde", "lw", "lx1", "lx2", "cp", "outs", "loc",
              "ad1", "ad2", "ad3", "hop10", "hop11", "hop20", "hop21", "hop30", "hop31", "hop4", "bg1", "bg2"]


def rank_program(g, core, T, topo):
    rank = T.rank_of(core)
    if rank is None:
        return
    V, S, PE, Y = g.vector, g.scalar, g.tensor, g.sync
    sem = T.sem
    peer = lambda d: T.cores[(rank + d) % NV]
    cnt = {"v": 0, "s": 0, "pe": 0, "gi": 0, "loc": 0}

    def done(name, ins):
        ins.then_inc(sem[name], 1)
        cnt[name] += 1
        return cnt[name]

    def vw(n):
        V.wait_ge(sem.v, n)

    def ts(out, in0, op, c, op1=None, c1=None):
        if op1 is None:
            return done("v", V.tensor_scalar(out=out, in0=in0, scalar1=c, scalar2=None, op0=op))
        return done("v", V.tensor_scalar(out=out, in0=in0, scalar1=c, scalar2=c1, op0=op, op1=op1))

    def tt(out, in0, in1, op=A.add):
        return done("v", V.tensor_tensor(out=out, in0=in0, in1=in1, op=op))

    def vcopy(out, in_):
        return done("v", V.tensor_copy(out=out, in_=in_))

    def fill(ap, c):
        return done("v", V.memset(ap, c))

    def act(out, in_, func=AF.Copy, bias=0.0, scale=1.0):
        return done("s", S.activation(out=out, in_=in_, func=func, bias=bias, scale=scale))

    def mm(out, lhsT, rhs, start, stop, count=True):
        ins = PE.matmul(out=out, lhsT=lhsT, rhs=rhs, start=start, stop=stop)
        return done("pe", ins) if count else 0

    def iota(ap, pattern, cm=0, base=0):
        return done("gi", g.iota(ap, pattern, base, cm, allow_small_or_imprecise_dtypes=True))

    def sel(out, in_, pattern, op, c, base, cm):
        return done("gi", g.affine_select(out, in_, pattern, op, c, base, cm))

    ps = [T["ps%d" % b] for b in range(8)]
    cols = lambda t, q: t[:, 512 * q:512 * q + 512]
    al = lambda name: T[name][:, :, :]

    Y.dma_start(out=T.lst[:, :], in_=T.nx[:]).then_inc(sem.ldl, 16)
    S.dma_start(out=T.base[32:64, :], in_=T.w[:]).then_inc(sem.lda, 16)
    Y.dma_start(out=T.base[0:32, :], in_=T.nx[:]).then_inc(sem.lda, 16)
    S.dma_start(out=T.ei[:, :], in_=T.e[:]).then_inc(sem.lde, 16)
    Y.dma_start(out=T.xi[:, :], in_=T.x[:]).then_inc(sem.lde, 16)

    v_z = fill(T.w0[:, 0:256], 0)
    v_lr = fill(T.lrb[0:68, :, :, :], 0.0)
    v_w0 = fill(T.w0[:, 256:ZC], 0)
    S.wait_ge(sem.v, v_z)
    for c in range(ZC, 2048, 256):
        s_w0 = act(T.w0[:, c:c + 256], T.w0[:, 0:256])
    Y.wait_ge(sem.v, v_w0)
    Y.wait_ge(sem.s, s_w0)
    Y.dma_start(out=T.w0[1:128:16, :], in_=T.nx[:]).then_inc(sem.lw, 16)
    Y.dma_start(out=T.w0[8:128:16, :], in_=T.w[:]).then_inc(sem.lw, 16)
    g_b = iota(T.base[64:68, :], [[1, 512]], 512)

    V.wait_ge(sem.ldl, 16)
    v_l = vcopy(T.l1[:, :], T.lst[:, :])
    V.wait_ge(sem.lda, 32)
    V.wait_ge(sem.gi, g_b)
    v_b = vcopy(T.b16[0:68, 0:256], T.base[0:68, 0:256])
    S.wait_ge(sem.lda, 32)
    S.wait_ge(sem.gi, g_b)
    s_b = act(T.b16[0:68, 256:512], T.base[0:68, 256:512])

    fill(al("sh1"), 0.0)
    n = fill(T.rr[:, :], 0.0)
    vw(n)
    v_rr = fill(T.rr[:, 15:144:16], 1.0)
    v_s2 = fill(al("sh2"), 0.0)
    V.wait_ge(sem.lde, 32)
    v_eu = vcopy(T.eu[:, :], T.ei[:, :])
    S.wait_ge(sem.v, v_rr)
    for name in ("sh4", "zz"):
        act(al(name), T.rr[:, 0:128], AF.Copy, 0.0, 0.0)
    s_c = act(al("one"), T.rr[:, 0:128], AF.Copy, 1.0, 0.0)

    g.wait_ge(sem.v, v_lr)
    for rows, r0, r1, pattern in (((0, 32), 1, 2, [[-1, 4], [-4, 8], [0, 1]]),
                                  ((64, 68), 0, 1, [[-1, 4], [0, 8], [0, 1]]),
                                  ((32, 64), 8, 16, [[-1, 4], [-4, 8], [0, 8]])):
        g.wait_ge(sem.gi, cnt["gi"])
        ap = T.lrb[rows[0]:rows[1], :, :, r0:r1]
        g_lr = sel(ap, ap, pattern, A.not_equal, 1.0, 0, 1)
    g.wait_ge(sem.gi, g_lr)

    def shifts(m):
        sh = T["sh%d" % m]
        k = 8 + 2 * m if m > 1 else 9
        for r0, r1 in ((m + 1, min(2 * m + 1, 8)), (8 + m, k)):
            if r1 > r0:
                n = sel(sh[:, :, r0:r1], sh[:, :, r0:r1], [[-16, 8], [-1, r1 - r0]], A.not_equal, 1.0, m - r0, 1)
        if k < 16:
            n = sel(sh[:, :, k:16], sh[:, :, k:16], [[-16, 8], [0, 16 - k]], A.not_equal, 1.0, -7 - m, 1)
        return n

    g.wait_ge(sem.v, v_rr)
    g_sh = {1: shifts(1)}
    g.wait_ge(sem.v, v_s2)
    g_sh[2] = shifts(2)
    g.wait_ge(sem.s, s_c)
    g_ht = iota(T.ht[:, :], [[2048, 2], [0, 8]])
    sel(T.rep[0:16, :, :], T.zz[0:16, :, :], [[0, 8], [1, 16]], A.not_equal, 1.0, 0, -1)
    n = sel(T.m16[0:16, :, :], T.zz[0:16, 0:2, 0:8], [[0, 2], [1, 8]], A.not_equal, 1.0, 0, -1)
    g.wait_ge(sem.gi, n)
    n = sel(T.m16[0:16, :, 1:8], T.m16[0:16, :, 1:8], [[0, 2], [1, 7]], A.not_equal, 1.0, 8, -1)
    g.wait_ge(sem.gi, n)
    g_m = sel(T.m16[0:16, 1:2, :], T.m16[0:16, 1:2, :], [[0, 1], [0, 8]], A.not_equal, 1.0, 15, -1)
    g_sh[4] = shifts(4)
    g_y = sel(T.y4[:, :], T.rr[:, :], [[-16, 9], [0, 16]], A.is_equal, 0.0, -4, 1)

    def send(out, src, d, name):
        dst = peer(d)
        rid, pid = topo.addr(dst, core)
        g.remote_dma(out, src, sem[name], sem.loc, pid, rid, topo.mask(core, dst))
        cnt["loc"] += len(topo.engines(core, dst))

    def landed(d):
        return len(topo.engines(peer(-d), core))

    g.wait_ge(sem.v, v_eu)
    for t in (1, 2, 3):
        send(T["le%d" % t][:, :], T.eu[:, 16 * t:min(16 * t + 32, 64)], t, "ad%d" % t)

    tabs = {1: (T.w0, T.tb), 2: (T.tb, T.ta), 4: (T.ta, T.win)}
    lists = {1: T.l1, 2: T.l2, 4: T.l4}
    gs = {1: T.g1, 2: T.g2, 4: T.g3}
    banks = {1: (0, 1, 2, 3), 2: (0, 1, 5, 7), 4: (0, 1, 2, 3)}
    mine = {1: (0, 1), 2: (0, 1), 4: (0, 2, 1)}
    v_ev, s_ev = v_w0, s_w0
    for m in (1, 2, 4):
        old, new = tabs[m]
        G, L, sh, bank = gs[m], lists[m], al("sh%d" % m), [ps[b] for b in banks[m]]
        ind = lambda q: old[:, 0:2048].indirect(L[:, 32 * q:32 * q + 32])
        if m == 1:
            V.wait_ge(sem.lw, 32)
            S.wait_ge(sem.lw, 32)
        vw(max(v_ev, v_l))
        V.wait_ge(sem.s, s_ev)
        S.wait_ge(sem.v, max(v_ev, v_l))
        S.wait_ge(sem.s, s_ev)
        got = {}
        for q in (0, 2):
            got[q] = vcopy(cols(G, q), ind(q))
        for q in (1, 3):
            got[q] = act(cols(G, q), ind(q))
        if m < 4:
            Y.wait_ge(sem.v, got[2])
            Y.wait_ge(sem.s, got[3])
            Y.dma_start(out=T["lf%d" % m][:, :], in_=G[m:128:16, :]).then_inc(sem["lx%d" % m], 16)

        if m == 1:
            PE.wait_ge(sem.v, v_b)
            PE.wait_ge(sem.s, s_b)
            PE.wait_ge(sem.gi, g_lr)
        for q in (0, 2, 1, 3):
            if m == 1 or q not in mine[m]:
                mm(bank[q][:, :], T.lrb[0:68, q, :, :], T.b16[0:68, :], True, False, False)

        def moves(m, q, f, lhsT, out, start, stop):
            G = gs[m]
            n = 0
            if m == 1:
                todo = [(out[:, 128 * (i % 4) + 64 * f:128 * (i % 4) + 64 * f + 64], G[:, 1024 * f + i:1024 * f + 1024:16])
                        for i in range(4 * q, 4 * q + 4)]
            elif m == 2:
                todo = [(out[:, x:512:8], G[:, 256 * x + 64 * q:256 * x + 64 * q + 64]) for x in range(4 * f, 4 * f + 4)]
            else:
                todo = [(out[:, :], G[:, 1024 * f + q // 2:1024 * f + 1024:2])] if q % 2 == f else []
            for i, (o, r) in enumerate(todo):
                last = stop and i == len(todo) - 1
                n = mm(o, lhsT, r, start and i == 0, last, last)
            return n

        for q in range(4):
            if m > 1 and q not in mine[m]:
                for k in (1, 2):
                    if k < m:
                        for f in (0, 1):
                            moves(k, q, f, al("sh%d" % k), bank[q], False, False)
        PE.wait_ge(sem.gi, g_sh[m])
        pc = {}
        for f in (0, 1):
            PE.wait_ge(sem.v, got[2 * f])
            PE.wait_ge(sem.s, got[2 * f + 1])
            for q in (0, 2, 1, 3):
                fresh = m > 1 and q in mine[m]
                n = moves(m, q, f, sh, bank[q], fresh and (f == 0 or m == 4), f == 1 or m == 4)
                if n:
                    pc[q] = n
        if m == 4:
            s_nf = act(T.nfar[0:16, :], T.b16[0:16, 0:256], AF.Copy, -FAR, 0.0)
            S.wait_ge(sem.gi, g_ht)
            S.wait_ge(sem.v, v_eu)
            s_hx = {0: act(T.hx0[:, :], T.ht[:, :].indirect(T.eu[:, 16:32])), 3: 0}
        for q in mine[m]:
            V.wait_ge(sem.pe, pc[q])
            v_ev = tt(cols(new, q), cols(old, q), bank[q][:, :]) if m > 1 else vcopy(cols(new, q), bank[q][:, :])
        for q in range(4):
            if q not in mine[m]:
                S.wait_ge(sem.pe, pc[q])
                s_ev = act(cols(new, q), bank[q][:, :])
        if m < 4:
            V.wait_ge(sem["lx%d" % m], 16)
            v_l = vcopy(lists[2 * m][:, :], T["lf%d" % m][:, :])
        if m == 1:
            PE.wait_ge(sem.gi, g_m)
            p_mt = mm(ps[6][:, 0:16], T.rep[0:16, :, :], T.m16[0:16, :, :], True, True)

    PE.wait_ge(sem.gi, g_y)
    for h in (0, 1):
        for b in range(16):
            px = mm(ps[4][:, 64 * h:64 * h + 64], T.y4[:, 15 - b:143 - b], T.g3[:, 2 * b + h:2048:32], b == 0, b == 15, b == 15)

    V.wait_ge(sem.pe, p_mt)
    v_mt = vcopy(T.mt[:, :], ps[6][:, 0:16])
    n = ts(T.hi0[:, :], T.ei[:, 0:16], A.is_ge, 8, A.mult, 2048.0)
    vw(n)
    n = tt(T.xo[:, :], T.xi[:, :], T.hi0[:, :])
    vw(n)
    vcopy(T.off0[:, :], T.xo[:, :])
    S.wait_ge(sem.v, v_mt)
    act(T.mk0[:, 0:128], T.mt[:, :].indirect(T.eu[:, 0:8]))
    V.wait_ge(sem.pe, px)
    v_l = vcopy(T.l8[:, :], ps[4][:, 0:128])

    n = sel(al("s1"), al("one"), [[16, 8], [0, 16]], A.is_ge, 0.0, 7, -1)
    n2 = iota(T.sd[:, :], [[0, 256]])
    sel(al("idn"), al("zz"), [[-16, 8], [-1, 16]], A.not_equal, 1.0, 0, 1)
    g.wait_ge(sem.gi, n)
    sel(al("sums"), al("s1"), [[-16, 8], [0, 16]], A.is_ge, 0.0, 0, 1)
    g.wait_ge(sem.gi, n2)
    sel(T.sd[:, :], T.sd[:, :], [[0, 16], [1, 16]], A.not_equal, -BIG, 0, 0)
    n = sel(al("w1"), al("one"), [[16, 8], [0, 16]], A.is_ge, 0.0, 15, -1)
    g.wait_ge(sem.s, s_nf)
    g_v = sel(T.far[0:16, :], T.nfar[0:16, :], [[0, 16], [1, 16]], A.not_equal, 0.0, 0, -1)
    g.wait_ge(sem.gi, n)
    sel(al("sumw"), al("w1"), [[-16, 8], [0, 16]], A.is_ge, 0.0, -8, 1)
    g_w = sel(T.repf[0:16, :, :], T.zz[0:16, :, :], [[0, 8], [1, 16]], A.not_equal, 64.0, 0, -1)

    win = T.win[:, 0:4096]
    vw(max(v_ev, v_l))
    V.wait_ge(sem.s, s_ev)
    S.wait_ge(sem.v, v_l)
    S.wait_ge(sem.s, s_ev)
    n = vcopy(T.win[:, 2048:2048 + CUT], T.win[:, 0:2048].indirect(T.l8[:, 0:CUT // 16]))
    s_w = act(T.win[:, 2048 + CUT:4096], T.win[:, 0:2048].indirect(T.l8[:, CUT // 16:128]))
    vw(n)
    V.wait_ge(sem.s, s_w)

    s_mk = {0: act(T.mk0[:, 128:256], T.mt[:, :].indirect(T.eu[:, 8:16]))}
    for t in (1, 2, 3):
        S.wait_ge(sem["ad%d" % t], landed(t))
        le = T["le%d" % t]
        s_mk[t] = act(T["mk%d" % t][:, :], T.mt[:, :].indirect(le[:, 0:16]))
        if t < 3:
            s_hx[t] = act(T["hx%d" % t][:, :], T.ht[:, :].indirect(le[:, 16:32]))

    half = lambda t, h: t[:, 128 * h:128 * h + 128]
    part = lambda t, h: t[:, 8 * h:8 * h + 8]

    def visit(t, v_free):
        off = T["land%d" % t] if t else T.off0
        M, mk, fin = T["mm%d" % t], T["mk%d" % t], t == 3
        if t:
            V.wait_ge(sem.s, s_mk[t])
        if t == 1:
            V.wait_ge(sem.cp, 16)
        vg = []
        for h in (0, 1):
            if t:
                V.wait_ge(sem["hop%d%d" % (t, h)], landed(1))
            elif h:
                V.wait_ge(sem.s, s_mk[0])
            vg.append(tt(half(M, h), win.indirect(part(off, h)), half(mk, h), A.mult))
        PE.wait_ge(sem.v, v_free)
        PE.wait_ge(sem.gi, g_v if t == 0 else g_w)
        PE.wait_ge(sem.s, s_hx[t])
        for h in (0, 1):
            mm(ps[6 + h][:, 0:128], (T.repf if fin else T.rep)[0:16, :, :], T.far[0:16, 0:128], True, False, False)
            if not fin:
                mm(ps[6 + h][:, 0:128], al("idn"), half(T["hx%d" % t], h), False, False, False)
        pr = []
        for h in (0, 1):
            PE.wait_ge(sem.v, vg[h])
            pr.append(mm(ps[6 + h][:, 0:128], al("sumf" if fin else "sums"), half(M, h), False, True))
        out = T.fo if fin else T["ho%d" % t]
        if t == 0:
            V.wait_ge(sem.gi, g_v)
        for h in (0, 1):
            V.wait_ge(sem.pe, pr[h])
            n = done("v", V.tensor_tensor_scan(out=half(T.sc, h), data0=T.sd[:, 0:128],
                                               data1=ps[6 + h][:, 0:128], initial=0.0, op0=A.add, op1=A.max))
            vw(n)
            c = vcopy(part(out, h), T.sc[:, 128 * h + 15:128 * h + 128:16])
            if not fin:
                g.wait_ge(sem.v, c)
                send(part(T["land%d" % (t + 1)], h), part(out, h), 1, "hop%d%d" % (t + 1, h))
        return vg[1], c

    def weights(t, M, n, v_free):
        PE.wait_ge(sem.v, max(n, v_free))
        mm(ps[4][:, 0:256], T.rep[0:16, :, :], T.far[0:16, :], True, False, False)
        p = mm(ps[4][:, 0:256], al("sumw"), M[:, :], False, True)
        V.wait_ge(sem.pe, p)
        n = done("v", V.tensor_tensor_scan(out=T.sw[:, :], data0=T.sd[:, :], data1=ps[4][:, 0:256],
                                           initial=0.0, op0=A.add, op1=A.max))
        vw(n)
        return n, vcopy(T["wl%d" % t][:, :], T.sw[:, 15:256:16])

    def report(t, n):
        g.wait_ge(sem.v, n)
        send(T["wr%d" % t][:, :], T["wl%d" % t][:, :], -t, "bg%d" % t)

    vg, c = visit(0, v_l)
    Y.wait_ge(sem.v, vg)
    Y.dma_start(out=T.win[15:128:16, 2048:4096], in_=T.win[15:128:16, 0:2048]).then_inc(sem.cp, 16)
    S.wait_ge(sem.cp, 16)
    s_gw = act(T.gw[:, :], win.indirect(T.off0[:, :]))
    V.wait_ge(sem.gi, g_w)
    n = ts(al("f512"), al("sums"), A.mult, 512.0)
    vw(n)
    v_sf = tt(al("sumf"), al("f512"), al("sumw"))

    vg, c = visit(1, c)
    v_w, n = weights(1, T.mm1, vg, 0)
    report(1, n)

    vg, c = visit(2, c)
    v_w, n = weights(2, T.mm2, vg, v_w)
    report(2, n)
    V.wait_ge(sem.s, s_gw)
    v_m = tt(T.mw0[:, :], T.gw[:, :], T.mk0[:, :], A.mult)

    vg, c = visit(3, max(c, v_sf))
    g.wait_ge(sem.v, c)
    send(T.fin[:, :], T.fo[:, :], 1, "hop4")

    v_w, n = weights(0, T.mw0, v_m, v_w)
    V.wait_ge(sem.bg1, landed(-1))
    V.wait_ge(sem.bg2, landed(-2))
    n1 = tt(T.acc1[:, :], T.wr1[:, :], T.wr2[:, :])
    vw(n1)
    vw(tt(T.acc[:, :], T.acc1[:, :], T.wl0[:, :]))

    V.wait_ge(sem.hop4, landed(1))
    n1 = ts(T.ft[:, :], T.fin[:, :], A.bitwise_and, 511)
    n2 = ts(T.fp[:, :], T.fin[:, :], A.arith_shift_right, 9)
    vw(n1)
    v_t = tt(T.ot[:, :], T.ft[:, :], T.acc[:, :])
    S.wait_ge(sem.v, n2)
    n = act(T.ol[:, :], T.fp[:, :])
    S.wait_ge(sem.s, n)
    S.dma_start(out=T.last[:], in_=T.ol[:, :]).then_inc(sem.outs, 16)
    Y.wait_ge(sem.v, v_t)
    Y.dma_start(out=T.total[:], in_=T.ot[:, :]).then_inc(sem.outs, 16)

    for name in ("loc", "v", "s", "pe", "gi"):
        g.wait_ge(sem[name], cnt[name])
    for name, n in (("outs", 32), ("lw", 32), ("cp", 16), ("lx1", 16), ("lx2", 16), ("lda", 32), ("ldl", 16), ("lde", 32)):
        g.wait_ge(sem[name], n)
